import numpy as np
import ml_dtypes


def mxq(x, axis, fmt="e4m3"):
    dtype, down = {"e4m3": (ml_dtypes.float8_e4m3fn, 7), "e5m2": (ml_dtypes.float8_e5m2, 14)}[fmt]
    v = np.moveaxis(np.asarray(x, np.float32).astype(ml_dtypes.bfloat16).astype(np.float64), axis, -1)
    blocks = v.reshape(v.shape[:-1] + (-1, 32))
    amax = np.abs(blocks).max(-1, keepdims=True)
    byte = np.maximum(np.where(amax > 0, np.frexp(amax)[1] - 1 + 127, 0) - down, 1)
    scale = np.exp2(byte - 127.0)
    codes = (blocks / scale).astype(np.float32).astype(dtype).astype(np.float64)
    return np.moveaxis((codes * scale).reshape(v.shape), -1, axis)


WIDE = False


def mx_kscale(k):
    if not WIDE:
        return np.ones(k)
    levels = np.array([10, -10, 5, -5, 0])
    if k % 512:
        return np.exp2(np.random.permutation(np.resize(levels, k // 32))).repeat(32)
    a = np.empty((k // 512, 16))
    for p in range(k // 512):
        a[p, :8] = np.random.permutation(np.resize(levels, 8))
        for g in range(8):
            far = levels[np.abs(levels - a[p, g]) >= 10]
            a[p, g + 8] = far[np.random.randint(len(far))]
    return np.exp2(a.ravel()).repeat(32)


BF16 = ml_dtypes.bfloat16


def bf(x):
    return np.asarray(x, np.float32).astype(BF16)


def f64(x):
    return np.asarray(x).astype(np.float64)


E2M1 = np.array([0.0, 0.5, 1.0, 1.5, 2.0, 3.0, 4.0, 6.0, -0.0, -0.5, -1.0, -1.5, -2.0, -3.0, -4.0, -6.0])


def pack_weight(w, fmt):
    k, n = w.shape
    w = f64(bf(w)).reshape(k // 32, 32, n)
    amax = np.abs(w).max(1)
    if fmt == "e4m3":
        byte = np.frexp(amax)[1] - 1 + 127 - 7
    else:
        mant, ex = np.frexp(amax / 6.0)
        byte = np.where(mant > 0.5, ex, ex - 1) + 127
    byte = np.clip(np.where(amax > 0, byte, 1), 1, 254)
    scaled = (w * np.exp2(127.0 - byte)[:, None, :]).reshape(k, n).astype(np.float32)
    by_word = np.ascontiguousarray(scaled.reshape(k // 512, 128, 4, n).transpose(0, 1, 3, 2))
    if fmt == "e4m3":
        words = by_word.astype(ml_dtypes.float8_e4m3fn).view(np.uint8)
    else:
        c = by_word.astype(ml_dtypes.float4_e2m1fn).view(np.uint8) & 0xF
        words = c[..., 0::2] | (c[..., 1::2] << 4)
    return np.ascontiguousarray(words), np.ascontiguousarray(byte.astype(np.uint8).reshape(k // 512, 16, n))


def unpack_weight(words, scales, fmt):
    g, p, n, _ = words.shape
    if fmt == "e4m3":
        vals = np.ascontiguousarray(words).view(ml_dtypes.float8_e4m3fn).astype(np.float64)
    else:
        nib = np.empty((g, p, n, 4), np.uint8)
        nib[..., 0::2] = words & 0xF
        nib[..., 1::2] = words >> 4
        vals = E2M1[nib]
    vals = vals * np.repeat(np.exp2(scales.astype(np.float64) - 127.0), 8, axis=1)[..., None]
    return vals.transpose(0, 1, 3, 2).reshape(g * 512, n)

def planes(Y):
    n, m = Y.shape
    b = f64(bf(Y)).reshape(n // 32, 32, m)
    amax = np.abs(b).max(1)
    byte = np.clip(np.where(amax > 0, np.frexp(amax)[1] - 1 + 127 - 7, 1), 1, 254)
    codes = (b * np.exp2(127.0 - byte)[:, None, :]).reshape(n, m).astype(np.float32).astype(ml_dtypes.float8_e4m3fn).view(np.uint8)
    words = codes.reshape(n // 512, 128, 4, m).transpose(0, 1, 3, 2)
    return np.ascontiguousarray(words), np.ascontiguousarray(byte.astype(np.uint8).reshape(n // 512, 16, m))


T, N, R, O = 1024, 1024, 512, 512


def setup_inputs():
    s, t = mx_kscale(N), mx_kscale(R)
    x = bf(np.random.standard_normal((T, N)) * s)
    a_words, a_scales = pack_weight(np.random.standard_normal((N, R)) / np.sqrt(N) / s[:, None], "e4m3")
    b_words, b_scales = pack_weight(np.random.standard_normal((N, R)) / np.sqrt(N) / s[:, None] * t, "e4m3")
    h1_words, h1_scales = pack_weight(np.random.standard_normal((N, O)) / np.sqrt(N) / s[:, None], "e4m3")
    h2_words, h2_scales = pack_weight(np.random.standard_normal((R, O)) / np.sqrt(R) / t[:, None], "e4m3")
    h3_words, h3_scales = pack_weight(0.5 * np.random.standard_normal((R, O)) / np.sqrt(R) / t[:, None], "e4m3")
    return {
        "x": x,
        "a_words": a_words,
        "a_scales": a_scales,
        "b_words": b_words,
        "b_scales": b_scales,
        "h1_words": h1_words,
        "h1_scales": h1_scales,
        "h2_words": h2_words,
        "h2_scales": h2_scales,
        "h3_words": h3_words,
        "h3_scales": h3_scales,
    }


def core(x, a_words, a_scales, b_words, b_scales, h1_words, h1_scales, h2_words, h2_scales, h3_words, h3_scales):
    xq = mxq(f64(x), 1, "e4m3")
    p = xq @ unpack_weight(a_words, a_scales, "e4m3")
    q = xq @ unpack_weight(b_words, b_scales, "e4m3")
    k2 = p * q
    k3 = p * k2
    y1 = xq @ unpack_weight(h1_words, h1_scales, "e4m3")
    y2 = mxq(k2, 1, "e4m3") @ unpack_weight(h2_words, h2_scales, "e4m3")
    y3 = mxq(k3, 1, "e4m3") @ unpack_weight(h3_words, h3_scales, "e4m3")
    return y1 + y2 + y3


def reference(x, a_words, a_scales, b_words, b_scales, h1_words, h1_scales, h2_words, h2_scales, h3_words, h3_scales):
    R_out = core(x, a_words, a_scales, b_words, b_scales, h1_words, h1_scales, h2_words, h2_scales, h3_words, h3_scales)
    words, scales = planes(R_out)
    return R_out, words, scales

@@ -1,0 +1,445 @@
+from contextlib import ExitStack
+
+import concourse.mybir as mybir
+from concourse.masks import make_identity
+
+F32 = mybir.dt.float32
+BF16 = mybir.dt.bfloat16
+I32 = mybir.dt.int32
+U8 = mybir.dt.uint8
+FP8X4 = mybir.dt.float8_e4m3fn_x4
+MULT = mybir.AluOpType.mult
+
+T, N, R, O = 1024, 1024, 512, 512
+FLOPS = 2 * T * (N * R * 2 + N * O + R * O * 2)
+P = 128
+PACK = 4
+KP = 512
+PERMUTED_FROM = 4
+
+
+def tile_factoredcubicvolterraequalizer_x2_kernel(
+    tc, x, a_words, a_scales, b_words, b_scales, h1_words, h1_scales,
+    h2_words, h2_scales, h3_words, h3_scales, out_0, out_1, out_2,
+):
+    nc = tc.nc
+    with ExitStack() as ctx:
+        keep = ctx.enter_context(tc.tile_pool(name="keep", bufs=1))
+        work = ctx.enter_context(tc.tile_pool(name="work", bufs=4))
+        psum = ctx.enter_context(tc.psum_pool(name="psum", bufs=8))
+        ctx.enter_context(tc.manual_schedule())
+
+        ident = keep.tile([P, P], F32, align_bytes=64)
+        raw_both = keep.tile([P, 2, 512], U8, align_bytes=64)
+        raw_pl = [raw_both[:, i, :] for i in range(2)]
+        perm_pl = [keep.tile([P, 512], U8, align_bytes=64, name="perm_pl%d" % i) for i in range(2)]
+        h_pl = keep.tile([P, 512], U8, align_bytes=64)
+        a_raw = keep.tile([P, 2, 512], I32, align_bytes=64)
+        b_raw = keep.tile([P, 2, 512], I32, align_bytes=64)
+        a_cod = keep.tile([P, 2, 512], I32, align_bytes=64)
+        b_cod = keep.tile([P, 2, 512], I32, align_bytes=64)
+        h_cod = keep.tile([P, 4, 512], I32, align_bytes=64)
+        x_raw = []
+        for c in range(2):
+            x_one = keep.tile([P, 1, N], BF16, align_bytes=64, name="x_one%d" % c)
+            x_raw.append((x_one, 0))
+        for c in range(2, 8, 2):
+            x_two = keep.tile([P, 2, N], BF16, align_bytes=64, name="x_two%d" % c)
+            x_raw.extend([(x_two, 0), (x_two, 1)])
+        x_cod = [keep.tile([P, 2, 256], I32, align_bytes=64, name="x_cod%d" % d) for d in range(4)]
+        x_pl = [keep.tile([P, 2, 256], U8, align_bytes=64, name="x_pl%d" % d) for d in range(4)]
+        xb = [keep.tile([P, 2, 256, 4], BF16, align_bytes=64, name="xb%d" % d) for d in range(4)]
+        x_perm = [keep.tile([P, 2, 512], F32, align_bytes=64, name="x_perm%d" % i) for i in range(2)]
+        psb = [keep.tile([P, 2, 256, 2], F32, align_bytes=64, name="psb%d" % d) for d in range(4)]
+        k2f = [keep.tile([P, 2, 256, 2], F32, align_bytes=64, name="k2f%d" % d) for d in range(4)]
+        k_cod = [keep.tile([P, 256], I32, align_bytes=64, name="k_cod%d" % c) for c in range(8)]
+        k_pl = [keep.tile([P, 256], U8, align_bytes=64, name="k_pl%d" % c) for c in range(8)]
+        y_sb = [keep.tile([P, 4, 512], F32, align_bytes=64, name="y_sb%d" % g) for g in range(2)]
+        y_cod = [keep.tile([P, 512], I32, align_bytes=64, name="y_cod%d" % g) for g in range(2)]
+        y_pl = [keep.tile([P, 512], U8, align_bytes=64, name="y_pl%d" % g) for g in range(2)]
+
+        x_v = [x[512 * g : 512 * g + 512, :].rearrange("(p t) k -> p t k", t=4) for g in range(2)]
+        o_v = [out_0[512 * g : 512 * g + 512, :].rearrange("(p t) m -> p t m", t=4) for g in range(2)]
+
+        nc.vector.memset(raw_both[:].rearrange("p i n -> p (i n)").bitcast(I32), 0)
+        zero = keep.tile([P, 512], BF16, align_bytes=64)
+        warm_cod = keep.tile([P, P], I32, align_bytes=64)
+        warm_pl = keep.tile([P, P], U8, align_bytes=64)
+        nc.vector.memset(zero[:].bitcast(I32), 0)
+        nc.vector.quantize_mx(out=warm_cod[:].bitcast(FP8X4), scales=warm_pl[:], in_=zero[:])
+        nc.vector.memset(h_pl[:].bitcast(I32), 0)
+
+        def load_x(eng, c, count, k0=0, k1=N):
+            eng.dma_start(
+                out=x_raw[c][0][:, :, k0:k1], in_=x_v[c // 4][:, c % 4 : c % 4 + count, k0:k1]
+            )
+
+        def load_w(eng, tile_ap, words):
+            eng.dma_start(out=tile_ap, in_=words.rearrange("g p n t -> p g (n t)").bitcast(I32))
+
+        def load_s(eng, plane, row, scales, quadrants=range(4)):
+            passes = scales.shape[0]
+            for q in quadrants:
+                r0 = 32 * q + row
+                eng.dma_start(
+                    out=plane[r0 : r0 + 4 * passes, :].bitcast(I32),
+                    in_=scales[:, 4 * q : 4 * q + 4, :].bitcast(I32),
+                )
+
+        load_x(nc.sync, 0, 1)
+        load_s(nc.sync, raw_pl[0], 0, a_scales)
+        load_x(nc.sync, 1, 1)
+        load_x(nc.sync, 2, 2)
+        load_w(nc.sync, a_raw[:], a_words)
+        make_identity(nc, ident[:])
+        load_s(nc.sync, raw_pl[1], 0, b_scales)
+        load_w(nc.sync, b_raw[:], b_words)
+        load_x(nc.sync, 4, 2)
+        load_x(nc.sync, 6, 2)
+        load_w(nc.sync, h_cod[:, 0:2, :], h1_words)
+        load_s(nc.sync, h_pl, 0, h1_scales)
+        load_s(nc.sync, h_pl, 8, h2_scales)
+        load_s(nc.sync, h_pl, 12, h3_scales)
+        load_w(nc.sync, h_cod[:, 2:3, :], h2_words)
+        load_w(nc.sync, h_cod[:, 3:4, :], h3_words)
+
+        def bank(nm):
+            return psum.tile([P, 512], F32, tag="bank", name=nm)
+
+        xt, pb, qb, kb = {}, {}, {}, {}
+
+        def permute_words(i):
+            nc.vector.tensor_copy(
+                out=x_perm[i][:].rearrange("p s (g u k) -> p (s g) u k", g=2, u=2),
+                in_=x_raw[4 + 2 * i][0][:].bitcast(F32).rearrange("p s (g k u) -> p (s g) u k", g=2, u=2),
+            )
+
+        def transpose_x(c):
+            xt[c] = bank("xt")
+            for g in range(2):
+                for u in range(2):
+                    col = (2 * g + u) * P
+                    if c < PERMUTED_FROM:
+                        words = x_raw[c][0][:, x_raw[c][1], :].bitcast(F32)
+                        in_ = words[:, 256 * g + u : 256 * (g + 1) : 2]
+                    else:
+                        in_ = x_perm[(c - 4) // 2][:, c % 2, col : col + P]
+                    nc.tensor.transpose(xt[c][:, col : col + P], in_, ident[:])
+
+        def copy_x(c):
+            d, half = divmod(c, 2)
+            nc.scalar.copy(
+                out=xb[d][:, :, half * P : (half + 1) * P, :].rearrange("p g r e -> p g (r e)").bitcast(F32).rearrange("p g (r u) -> p g r u", u=2),
+                in_=xt[c][:].rearrange("p (g u r) -> p g r u", g=2, u=2),
+            )
+
+        def quant_x(d):
+            nc.vector.quantize_mx(
+                out=x_cod[d][:].rearrange("p g r -> p (g r)").bitcast(FP8X4),
+                scales=x_pl[d][:].rearrange("p g r -> p (g r)"),
+                in_=xb[d][:].rearrange("p g r e -> p (g r e)"),
+            )
+
+        def perm(cod, raw, t0, t1):
+            nc.vector.tensor_copy(
+                out=cod[:].rearrange("p g (t m) -> p g t m", t=4)[:, :, t0:t1, :],
+                in_=raw[:].rearrange("p g (m t) -> p g t m", t=4)[:, :, t0:t1, :],
+            )
+
+        def perm_scales(i):
+            nc.vector.tensor_copy(
+                out=perm_pl[i][:].rearrange("p (t m) -> p t m", t=4),
+                in_=raw_pl[i].rearrange("p (m t) -> p t m", t=4),
+            )
+
+        def stage1(d, h, cod, i, banks, nm):
+            banks[d, h] = bank(nm)
+            for j in range(2):
+                t = 2 * h + j
+                for g in range(2):
+                    nc.tensor.matmul_mx(
+                        out=banks[d, h][:, j * 256 : (j + 1) * 256],
+                        lhsT=cod[:, g, t * P : (t + 1) * P].bitcast(FP8X4),
+                        lhsT_scale=perm_pl[i][4 * g : P, t * P : (t + 1) * P],
+                        rhs=x_cod[d][:, g, :].bitcast(FP8X4),
+                        rhs_scale=x_pl[d][:, g, :],
+                        start=(g == 0),
+                        stop=(g == 1),
+                    )
+
+        def copy_p(d, h):
+            nc.scalar.copy(out=psb[d][:, h, :, :], in_=pb[d, h][:].rearrange("p (j n) -> p n j", j=2))
+
+        def make_k2(d, h):
+            nc.vector.tensor_tensor(
+                out=k2f[d][:, h, :, :],
+                in0=qb[d, h][:].rearrange("p (j n) -> p n j", j=2),
+                in1=psb[d][:, h, :, :],
+                op=MULT,
+            )
+
+        def tokens(tile, c):
+            d, half = divmod(c, 2)
+            return tile[d][:, :, half * P : (half + 1) * P, :].rearrange("p h n j -> p n h j")
+
+        def k_tile(c):
+            if c not in kb:
+                kb[c] = work.tile([P, 2, P, 2, 2], BF16, align_bytes=64, tag="kb", name="kb")
+            return kb[c]
+
+        def make_k3(c):
+            nc.vector.tensor_tensor(out=k_tile(c)[:, 1, :, :, :], in0=tokens(k2f, c), in1=tokens(psb, c), op=MULT)
+
+        def cast_k2(c):
+            nc.scalar.copy(out=k_tile(c)[:, 0, :, :, :], in_=tokens(k2f, c))
+
+        def quant_k(c):
+            nc.vector.quantize_mx(
+                out=k_cod[c][:].bitcast(FP8X4),
+                scales=k_pl[c][:],
+                in_=kb[c][:].rearrange("p i n h j -> p (i n h j)"),
+            )
+
+        def x_columns(tile, c, g):
+            d, half = divmod(c, 2)
+            return tile[d][:, g, half * P : (half + 1) * P]
+
+        def k_columns(tile, c, i):
+            return tile[c][:, i * P : (i + 1) * P]
+
+        stage2_operands = [
+            (x_columns, x_cod, x_pl, 0),
+            (x_columns, x_cod, x_pl, 1),
+            (k_columns, k_cod, k_pl, 0),
+            (k_columns, k_cod, k_pl, 1),
+        ]
+
+        def stage2(c, out_ap, m0, width, passes):
+            for i in passes:
+                columns, cod, pl, half = stage2_operands[i]
+                nc.tensor.matmul_mx(
+                    out=out_ap,
+                    lhsT=columns(cod, c, half).bitcast(FP8X4),
+                    lhsT_scale=columns(pl, c, half),
+                    rhs=h_cod[:, i, m0 : m0 + width].bitcast(FP8X4),
+                    rhs_scale=h_pl[4 * i : P, m0 : m0 + width],
+                    start=(i == 0),
+                    stop=(i == 3),
+                )
+
+        ybank, yb = {}, {}
+
+        def stage2_wide(c):
+            ybank[c] = bank("ybank")
+            stage2(c, ybank[c][:], 0, 512, range(4))
+
+        def copy_y(c):
+            g, t = divmod(c, 4)
+            nc.scalar.copy(out=y_sb[g][:, t, :], in_=ybank[c][:])
+
+        def store_y(c):
+            g, t = divmod(c, 4)
+            nc.sync.dma_start(out=o_v[g][:, t, :], in_=y_sb[g][:, t, :])
+
+        last = {}
+
+        def part_x(c, m0, w):
+            last[c, m0] = bank("last")
+            stage2(c, last[c, m0][:, :w], m0, w, range(2))
+
+        def part_k(c, m0, w):
+            stage2(c, last[c, m0][:, :w], m0, w, range(2, 4))
+
+        def copy_part(c, m0, w):
+            nc.scalar.copy(out=y_sb[c // 4][:, c % 4, m0 : m0 + w], in_=last[c, m0][:, :w])
+
+        def copy_part_v(c, m0, w):
+            nc.vector.tensor_copy(out=y_sb[c // 4][:, c % 4, m0 : m0 + w], in_=last[c, m0][:, :w])
+
+        def store_part(c, m0, w):
+            nc.sync.dma_start(out=o_v[c // 4][:, c % 4, m0 : m0 + w], in_=y_sb[c // 4][:, c % 4, m0 : m0 + w])
+
+        def interleave_y(g, m0, width, engine):
+            yb[g, m0] = work.tile([P, 1024], BF16, align_bytes=64, tag="yb", name="yb")
+            copy = nc.scalar.copy if engine == "scalar" else nc.vector.tensor_copy
+            copy(
+                out=yb[g, m0][:, : 4 * width].rearrange("p (m t) -> p m t", t=4),
+                in_=y_sb[g][:, :, m0 : m0 + width].rearrange("p t m -> p m t"),
+            )
+
+        def quant_y(g, m0, width):
+            nc.vector.quantize_mx(
+                out=y_cod[g][:, m0 : m0 + width].bitcast(FP8X4),
+                scales=y_pl[g][:, m0 : m0 + width],
+                in_=yb[g, m0][:, : 4 * width],
+            )
+
+        def store_codes(g, m0, width):
+            nc.sync.dma_start(
+                out=out_1[g].rearrange("p m t -> p (m t)")[:, 4 * m0 : 4 * (m0 + width)].bitcast(I32),
+                in_=y_cod[g][:, m0 : m0 + width],
+            )
+
+        def store_scales(g):
+            for q in range(4):
+                eng = nc.sync
+                eng.dma_start(
+                    out=out_2[g, 4 * q : 4 * q + 4, :].bitcast(I32), in_=y_pl[g][32 * q : 32 * q + 4, :].bitcast(I32)
+                )
+
+        def p_of(d, h):
+            stage1(d, h, a_cod, 0, pb, "pb")
+
+        def q_of(d, h):
+            stage1(d, h, b_cod, 1, qb, "qb")
+
+        def warm_up(count):
+            wb = bank("wb")
+            for i in range(count):
+                nc.tensor.matmul_mx(
+                    out=wb[:, 0:P],
+                    lhsT=warm_cod[:].bitcast(FP8X4),
+                    lhsT_scale=warm_pl[:],
+                    rhs=warm_cod[:].bitcast(FP8X4),
+                    rhs_scale=warm_pl[:],
+                    start=True,
+                    stop=True,
+                )
+
+        warm_up(8)
+        perm_scales(0)
+        transpose_x(0)
+        copy_x(0)
+        transpose_x(1)
+        copy_x(1)
+        quant_x(0)
+        warm_up(8)
+        perm(a_cod, a_raw, 0, 2)
+        transpose_x(2)
+        copy_x(2)
+        perm(a_cod, a_raw, 2, 4)
+        transpose_x(3)
+        copy_x(3)
+        quant_x(1)
+        warm_up(8)
+        perm_scales(1)
+        p_of(0, 0)
+        copy_p(0, 0)
+        perm(b_cod, b_raw, 0, 2)
+        p_of(0, 1)
+        copy_p(0, 1)
+        perm(b_cod, b_raw, 2, 4)
+        p_of(1, 0)
+        copy_p(1, 0)
+        permute_words(0)
+        p_of(1, 1)
+        copy_p(1, 1)
+        q_of(0, 0)
+        make_k2(0, 0)
+        q_of(0, 1)
+        make_k2(0, 1)
+        transpose_x(4)
+        copy_x(4)
+        permute_words(1)
+        transpose_x(5)
+        copy_x(5)
+        make_k3(0)
+        q_of(1, 0)
+        cast_k2(0)
+        quant_x(2)
+        q_of(1, 1)
+        cast_k2(1)
+        make_k2(1, 0)
+        transpose_x(6)
+        copy_x(6)
+        make_k2(1, 1)
+        transpose_x(7)
+        copy_x(7)
+        make_k3(1)
+        p_of(2, 0)
+        copy_p(2, 0)
+        quant_x(3)
+        p_of(2, 1)
+        copy_p(2, 1)
+        quant_k(0)
+        q_of(2, 0)
+        cast_k2(2)
+        make_k2(2, 0)
+        q_of(2, 1)
+        cast_k2(3)
+        make_k2(2, 1)
+        p_of(3, 0)
+        copy_p(3, 0)
+        quant_k(1)
+        p_of(3, 1)
+        copy_p(3, 1)
+        make_k3(2)
+        q_of(3, 0)
+        cast_k2(4)
+        make_k3(3)
+        q_of(3, 1)
+        cast_k2(5)
+        make_k2(3, 0)
+        stage2_wide(0)
+        copy_y(0)
+        make_k2(3, 1)
+        store_y(0)
+        stage2_wide(1)
+        cast_k2(6)
+        quant_k(2)
+        stage2_wide(2)
+        cast_k2(7)
+        quant_k(3)
+        stage2_wide(3)
+        copy_y(1)
+        make_k3(4)
+        store_y(1)
+        copy_y(2)
+        make_k3(5)
+        store_y(2)
+        copy_y(3)
+        quant_k(4)
+        store_y(3)
+        stage2_wide(4)
+        copy_y(4)
+        make_k3(6)
+        store_y(4)
+        quant_k(5)
+        stage2_wide(5)
+        copy_y(5)
+        make_k3(7)
+        part_x(6, 0, 256)
+        quant_k(6)
+        part_k(6, 0, 256)
+        copy_part(6, 0, 256)
+        quant_k(7)
+        part_x(7, 0, 256)
+        interleave_y(0, 0, 256, "vector")
+        part_k(7, 0, 256)
+        copy_part(7, 0, 256)
+        interleave_y(0, 256, 256, "vector")
+        part_x(6, 256, 256)
+        quant_y(0, 0, 256)
+        part_k(6, 256, 256)
+        copy_part(6, 256, 256)
+        quant_y(0, 256, 256)
+        store_codes(0, 0, 512)
+        part_x(7, 256, 128)
+        interleave_y(1, 0, 256, "vector")
+        store_scales(0)
+        part_k(7, 256, 128)
+        copy_part(7, 256, 128)
+        interleave_y(1, 256, 128, "vector")
+        store_y(5)
+        part_x(7, 384, 128)
+        quant_y(1, 0, 256)
+        store_part(6, 0, 512)
+        part_k(7, 384, 128)
+        copy_part(7, 384, 128)
+        interleave_y(1, 384, 128, "vector")
+        store_part(7, 0, 512)
+        quant_y(1, 256, 128)
+        store_codes(1, 0, 256)
+        quant_y(1, 384, 128)
+        store_codes(1, 256, 256)
+        store_scales(1)

@@ -13,9 +13,11 @@ MULT = mybir.AluOpType.mult
 T, N, R, O = 1024, 1024, 512, 512
 FLOPS = 2 * T * (N * R * 2 + N * O + R * O * 2)
 P = 128
-PACK = 4
-KP = 512
-PERMUTED_FROM = 4
+TILES = 8
+PAIRS = 4
+SORTED_FROM = 2
+WARM_UPS = 3
+END_PIECES = ((0, 256), (256, 128), (384, 128))
 
 
 def tile_factoredcubicvolterraequalizer_x2_kernel(
@@ -29,152 +31,176 @@ def tile_factoredcubicvolterraequalizer_x2_kernel(
         psum = ctx.enter_context(tc.psum_pool(name="psum", bufs=8))
         ctx.enter_context(tc.manual_schedule())
 
+        def kept(name, shape, dtype, count):
+            return [keep.tile(shape, dtype, align_bytes=64, name="%s%d" % (name, i)) for i in range(count)]
+
         ident = keep.tile([P, P], F32, align_bytes=64)
-        raw_both = keep.tile([P, 2, 512], U8, align_bytes=64)
-        raw_pl = [raw_both[:, i, :] for i in range(2)]
-        perm_pl = [keep.tile([P, 512], U8, align_bytes=64, name="perm_pl%d" % i) for i in range(2)]
-        h_pl = keep.tile([P, 512], U8, align_bytes=64)
-        a_raw = keep.tile([P, 2, 512], I32, align_bytes=64)
-        b_raw = keep.tile([P, 2, 512], I32, align_bytes=64)
-        a_cod = keep.tile([P, 2, 512], I32, align_bytes=64)
-        b_cod = keep.tile([P, 2, 512], I32, align_bytes=64)
-        h_cod = keep.tile([P, 4, 512], I32, align_bytes=64)
-        x_raw = []
-        for c in range(2):
-            x_one = keep.tile([P, 1, N], BF16, align_bytes=64, name="x_one%d" % c)
-            x_raw.append((x_one, 0))
-        for c in range(2, 8, 2):
-            x_two = keep.tile([P, 2, N], BF16, align_bytes=64, name="x_two%d" % c)
-            x_raw.extend([(x_two, 0), (x_two, 1)])
-        x_cod = [keep.tile([P, 2, 256], I32, align_bytes=64, name="x_cod%d" % d) for d in range(4)]
-        x_pl = [keep.tile([P, 2, 256], U8, align_bytes=64, name="x_pl%d" % d) for d in range(4)]
-        xb = [keep.tile([P, 2, 256, 4], BF16, align_bytes=64, name="xb%d" % d) for d in range(4)]
-        x_perm = [keep.tile([P, 2, 512], F32, align_bytes=64, name="x_perm%d" % i) for i in range(2)]
-        psb = [keep.tile([P, 2, 256, 2], F32, align_bytes=64, name="psb%d" % d) for d in range(4)]
-        k2f = [keep.tile([P, 2, 256, 2], F32, align_bytes=64, name="k2f%d" % d) for d in range(4)]
-        k_cod = [keep.tile([P, 256], I32, align_bytes=64, name="k_cod%d" % c) for c in range(8)]
-        k_pl = [keep.tile([P, 256], U8, align_bytes=64, name="k_pl%d" % c) for c in range(8)]
-        y_sb = [keep.tile([P, 4, 512], F32, align_bytes=64, name="y_sb%d" % g) for g in range(2)]
-        y_cod = [keep.tile([P, 512], I32, align_bytes=64, name="y_cod%d" % g) for g in range(2)]
-        y_pl = [keep.tile([P, 512], U8, align_bytes=64, name="y_pl%d" % g) for g in range(2)]
+        w_pl_raw = kept("w_pl_raw", [P, R], U8, 2)
+        w_pl = kept("w_pl", [P, R], U8, 2)
+        w_raw = kept("w_raw", [P, 2, R], I32, 2)
+        w_cod = kept("w_cod", [P, 2, R], I32, 2)
+        h_pl = keep.tile([P, O], U8, align_bytes=64)
+        h_cod = keep.tile([P, 4, O], I32, align_bytes=64)
+        x_one = kept("x_one", [P, 1, N], BF16, 4)
+        x_two = kept("x_two", [P, 2, N], BF16, 2)
+        x_sorted_one = kept("x_sorted_one", [P, 1, 512], F32, 2)
+        x_sorted_two = kept("x_sorted_two", [P, 2, 512], F32, 2)
+        xb_one = kept("xb_one", [P, 2, P, 4], BF16, 4)
+        xb_two = kept("xb_two", [P, 2, 2 * P, 4], BF16, 2)
+        x_cod = kept("x_cod", [P, 2, 256], I32, PAIRS)
+        x_pl = kept("x_pl", [P, 2, 256], U8, PAIRS)
+        p_sb = kept("p_sb", [P, 2, 256, 2], F32, PAIRS)
+        k2_sb = kept("k2_sb", [P, 2, 256, 2], F32, PAIRS)
+        kb = kept("kb", [P, 2, P, 2, 2], BF16, TILES)
+        k_cod = kept("k_cod", [P, 256], I32, TILES)
+        k_pl = kept("k_pl", [P, 256], U8, TILES)
+        y_sb = kept("y_sb", [P, 4, O], F32, 2)
+        y_cod = kept("y_cod", [P, O], I32, 2)
+        y_pl = kept("y_pl", [P, O], U8, 2)
+        zero = keep.tile([P, 512], BF16, align_bytes=64)
+        warm_cod = keep.tile([P, 512], I32, align_bytes=64)
+        warm_pl = keep.tile([P, 512], U8, align_bytes=64)
 
         x_v = [x[512 * g : 512 * g + 512, :].rearrange("(p t) k -> p t k", t=4) for g in range(2)]
         o_v = [out_0[512 * g : 512 * g + 512, :].rearrange("(p t) m -> p t m", t=4) for g in range(2)]
 
-        nc.vector.memset(raw_both[:].rearrange("p i n -> p (i n)").bitcast(I32), 0)
-        zero = keep.tile([P, 512], BF16, align_bytes=64)
-        warm_cod = keep.tile([P, P], I32, align_bytes=64)
-        warm_pl = keep.tile([P, P], U8, align_bytes=64)
+        for plane in (w_pl_raw[0], w_pl_raw[1], h_pl, warm_pl):
+            nc.vector.memset(plane[:].bitcast(I32), 0)
         nc.vector.memset(zero[:].bitcast(I32), 0)
-        nc.vector.quantize_mx(out=warm_cod[:].bitcast(FP8X4), scales=warm_pl[:], in_=zero[:])
-        nc.vector.memset(h_pl[:].bitcast(I32), 0)
+        nc.vector.memset(warm_cod[:], 0)
+        nc.vector.quantize_mx(out=warm_cod[:, 0:P].bitcast(FP8X4), scales=warm_pl[:, 0:P], in_=zero[:])
+        make_identity(nc, ident[:])
 
-        def load_x(eng, c, count, k0=0, k1=N):
-            eng.dma_start(
-                out=x_raw[c][0][:, :, k0:k1], in_=x_v[c // 4][:, c % 4 : c % 4 + count, k0:k1]
-            )
+        def load_words(tile_ap, words):
+            nc.sync.dma_start(out=tile_ap, in_=words.rearrange("g p n t -> p g (n t)").bitcast(I32))
 
-        def load_w(eng, tile_ap, words):
-            eng.dma_start(out=tile_ap, in_=words.rearrange("g p n t -> p g (n t)").bitcast(I32))
-
-        def load_s(eng, plane, row, scales, quadrants=range(4)):
+        def load_scales(plane, row, scales):
             passes = scales.shape[0]
-            for q in quadrants:
+            for q in range(4):
                 r0 = 32 * q + row
-                eng.dma_start(
+                nc.sync.dma_start(
                     out=plane[r0 : r0 + 4 * passes, :].bitcast(I32),
                     in_=scales[:, 4 * q : 4 * q + 4, :].bitcast(I32),
                 )
 
-        load_x(nc.sync, 0, 1)
-        load_s(nc.sync, raw_pl[0], 0, a_scales)
-        load_x(nc.sync, 1, 1)
-        load_x(nc.sync, 2, 2)
-        load_w(nc.sync, a_raw[:], a_words)
-        make_identity(nc, ident[:])
-        load_s(nc.sync, raw_pl[1], 0, b_scales)
-        load_w(nc.sync, b_raw[:], b_words)
-        load_x(nc.sync, 4, 2)
-        load_x(nc.sync, 6, 2)
-        load_w(nc.sync, h_cod[:, 0:2, :], h1_words)
-        load_s(nc.sync, h_pl, 0, h1_scales)
-        load_s(nc.sync, h_pl, 8, h2_scales)
-        load_s(nc.sync, h_pl, 12, h3_scales)
-        load_w(nc.sync, h_cod[:, 2:3, :], h2_words)
-        load_w(nc.sync, h_cod[:, 3:4, :], h3_words)
+        def load_x_one(c):
+            nc.sync.dma_start(out=x_one[c][:], in_=x_v[0][:, c : c + 1, :])
 
-        def bank(nm):
-            return psum.tile([P, 512], F32, tag="bank", name=nm)
+        def load_x_two(i):
+            nc.sync.dma_start(out=x_two[i][:], in_=x_v[1][:, 2 * i : 2 * i + 2, :])
 
-        xt, pb, qb, kb = {}, {}, {}, {}
+        load_x_one(0)
+        load_x_one(1)
+        load_scales(w_pl_raw[0], 0, a_scales)
+        load_words(w_raw[0][:], a_words)
+        load_x_one(2)
+        load_x_one(3)
+        load_scales(w_pl_raw[1], 0, b_scales)
+        load_words(w_raw[1][:], b_words)
+        load_x_two(0)
+        load_x_two(1)
+        load_words(h_cod[:, 0:2, :], h1_words)
+        load_words(h_cod[:, 2:3, :], h2_words)
+        load_words(h_cod[:, 3:4, :], h3_words)
+        load_scales(h_pl, 0, h1_scales)
+        load_scales(h_pl, 8, h2_scales)
+        load_scales(h_pl, 12, h3_scales)
 
-        def permute_words(i):
+        def bank(name):
+            return psum.tile([P, 512], F32, tag="bank", name=name)
+
+        xt, pq_bank, y_bank, yb = {}, {}, {}, {}
+
+        def sort_words(dst, src):
             nc.vector.tensor_copy(
-                out=x_perm[i][:].rearrange("p s (g u k) -> p (s g) u k", g=2, u=2),
-                in_=x_raw[4 + 2 * i][0][:].bitcast(F32).rearrange("p s (g k u) -> p (s g) u k", g=2, u=2),
+                out=dst[:].rearrange("p s (g u k) -> p (s g) u k", g=2, u=2),
+                in_=src[:].bitcast(F32).rearrange("p s (g k u) -> p (s g) u k", g=2, u=2),
             )
+
+        def sort_one(c):
+            sort_words(x_sorted_one[c - SORTED_FROM], x_one[c])
+
+        def sort_two(i):
+            sort_words(x_sorted_two[i], x_two[i])
 
         def transpose_x(c):
             xt[c] = bank("xt")
             for g in range(2):
                 for u in range(2):
                     col = (2 * g + u) * P
-                    if c < PERMUTED_FROM:
-                        words = x_raw[c][0][:, x_raw[c][1], :].bitcast(F32)
-                        in_ = words[:, 256 * g + u : 256 * (g + 1) : 2]
+                    if c < SORTED_FROM:
+                        in_ = x_one[c][:, 0, :].bitcast(F32)[:, 256 * g + u : 256 * (g + 1) : 2]
+                    elif c < 4:
+                        in_ = x_sorted_one[c - SORTED_FROM][:, 0, col : col + P]
                     else:
-                        in_ = x_perm[(c - 4) // 2][:, c % 2, col : col + P]
+                        in_ = x_sorted_two[(c - 4) // 2][:, c % 2, col : col + P]
                     nc.tensor.transpose(xt[c][:, col : col + P], in_, ident[:])
 
         def copy_x(c):
-            d, half = divmod(c, 2)
+            if c < 4:
+                dst = xb_one[c][:]
+            else:
+                dst = xb_two[(c - 4) // 2][:, :, (c % 2) * P : (c % 2 + 1) * P, :]
             nc.scalar.copy(
-                out=xb[d][:, :, half * P : (half + 1) * P, :].rearrange("p g r e -> p g (r e)").bitcast(F32).rearrange("p g (r u) -> p g r u", u=2),
+                out=dst.rearrange("p g r e -> p g (r e)").bitcast(F32).rearrange("p g (r u) -> p g r u", u=2),
                 in_=xt[c][:].rearrange("p (g u r) -> p g r u", g=2, u=2),
             )
 
-        def quant_x(d):
+        def quant_x_one(c):
+            d, half = divmod(c, 2)
+            for g in range(2):
+                nc.vector.quantize_mx(
+                    out=x_cod[d][:, g, half * P : (half + 1) * P].bitcast(FP8X4),
+                    scales=x_pl[d][:, g, half * P : (half + 1) * P],
+                    in_=xb_one[c][:, g, :, :].rearrange("p r e -> p (r e)"),
+                )
+
+        def quant_x_two(d):
             nc.vector.quantize_mx(
                 out=x_cod[d][:].rearrange("p g r -> p (g r)").bitcast(FP8X4),
                 scales=x_pl[d][:].rearrange("p g r -> p (g r)"),
-                in_=xb[d][:].rearrange("p g r e -> p (g r e)"),
+                in_=xb_two[d - 2][:].rearrange("p g r e -> p (g r e)"),
             )
 
-        def perm(cod, raw, t0, t1):
+        def deal_words(i, h):
             nc.vector.tensor_copy(
-                out=cod[:].rearrange("p g (t m) -> p g t m", t=4)[:, :, t0:t1, :],
-                in_=raw[:].rearrange("p g (m t) -> p g t m", t=4)[:, :, t0:t1, :],
+                out=w_cod[i][:].rearrange("p g (t m) -> p g m t", t=4)[:, :, :, 2 * h : 2 * h + 2],
+                in_=w_raw[i][:].rearrange("p g (m t) -> p g m t", t=4)[:, :, :, 2 * h : 2 * h + 2],
             )
 
-        def perm_scales(i):
+        def deal_scales(i):
             nc.vector.tensor_copy(
-                out=perm_pl[i][:].rearrange("p (t m) -> p t m", t=4),
-                in_=raw_pl[i].rearrange("p (m t) -> p t m", t=4),
+                out=w_pl[i][:].rearrange("p (t m) -> p t m", t=4),
+                in_=w_pl_raw[i][:].rearrange("p (m t) -> p t m", t=4),
             )
 
-        def stage1(d, h, cod, i, banks, nm):
-            banks[d, h] = bank(nm)
+        def project(i, d, h):
+            pq_bank[i, d, h] = bank("pq")
             for j in range(2):
                 t = 2 * h + j
                 for g in range(2):
                     nc.tensor.matmul_mx(
-                        out=banks[d, h][:, j * 256 : (j + 1) * 256],
-                        lhsT=cod[:, g, t * P : (t + 1) * P].bitcast(FP8X4),
-                        lhsT_scale=perm_pl[i][4 * g : P, t * P : (t + 1) * P],
+                        out=pq_bank[i, d, h][:, j * 256 : (j + 1) * 256],
+                        lhsT=w_cod[i][:, g, t * P : (t + 1) * P].bitcast(FP8X4),
+                        lhsT_scale=w_pl[i][4 * g : P, t * P : (t + 1) * P],
                         rhs=x_cod[d][:, g, :].bitcast(FP8X4),
                         rhs_scale=x_pl[d][:, g, :],
                         start=(g == 0),
                         stop=(g == 1),
                     )
 
-        def copy_p(d, h):
-            nc.scalar.copy(out=psb[d][:, h, :, :], in_=pb[d, h][:].rearrange("p (j n) -> p n j", j=2))
+        def p_of(d, h):
+            project(0, d, h)
+            nc.scalar.copy(out=p_sb[d][:, h, :, :], in_=pq_bank[0, d, h][:].rearrange("p (j n) -> p n j", j=2))
+
+        def q_of(d, h):
+            project(1, d, h)
 
         def make_k2(d, h):
             nc.vector.tensor_tensor(
-                out=k2f[d][:, h, :, :],
-                in0=qb[d, h][:].rearrange("p (j n) -> p n j", j=2),
-                in1=psb[d][:, h, :, :],
+                out=k2_sb[d][:, h, :, :],
+                in0=pq_bank[1, d, h][:].rearrange("p (j n) -> p n j", j=2),
+                in1=p_sb[d][:, h, :, :],
                 op=MULT,
             )
 
@@ -182,16 +208,11 @@ def tile_factoredcubicvolterraequalizer_x2_kernel(
             d, half = divmod(c, 2)
             return tile[d][:, :, half * P : (half + 1) * P, :].rearrange("p h n j -> p n h j")
 
-        def k_tile(c):
-            if c not in kb:
-                kb[c] = work.tile([P, 2, P, 2, 2], BF16, align_bytes=64, tag="kb", name="kb")
-            return kb[c]
-
         def make_k3(c):
-            nc.vector.tensor_tensor(out=k_tile(c)[:, 1, :, :, :], in0=tokens(k2f, c), in1=tokens(psb, c), op=MULT)
+            nc.vector.tensor_tensor(out=kb[c][:, 1, :, :, :], in0=tokens(k2_sb, c), in1=tokens(p_sb, c), op=MULT)
 
-        def cast_k2(c):
-            nc.scalar.copy(out=k_tile(c)[:, 0, :, :, :], in_=tokens(k2f, c))
+        def round_k2(c):
+            nc.scalar.copy(out=kb[c][:, 0, :, :, :], in_=tokens(k2_sb, c))
 
         def quant_k(c):
             nc.vector.quantize_mx(
@@ -200,69 +221,35 @@ def tile_factoredcubicvolterraequalizer_x2_kernel(
                 in_=kb[c][:].rearrange("p i n h j -> p (i n h j)"),
             )
 
-        def x_columns(tile, c, g):
+        def respond(c, m0, width):
             d, half = divmod(c, 2)
-            return tile[d][:, g, half * P : (half + 1) * P]
-
-        def k_columns(tile, c, i):
-            return tile[c][:, i * P : (i + 1) * P]
-
-        stage2_operands = [
-            (x_columns, x_cod, x_pl, 0),
-            (x_columns, x_cod, x_pl, 1),
-            (k_columns, k_cod, k_pl, 0),
-            (k_columns, k_cod, k_pl, 1),
-        ]
-
-        def stage2(c, out_ap, m0, width, passes):
-            for i in passes:
-                columns, cod, pl, half = stage2_operands[i]
+            y_bank[c, m0] = bank("y")
+            stationary = [
+                (x_cod[d][:, g, half * P : (half + 1) * P], x_pl[d][:, g, half * P : (half + 1) * P]) for g in range(2)
+            ] + [(k_cod[c][:, i * P : (i + 1) * P], k_pl[c][:, i * P : (i + 1) * P]) for i in range(2)]
+            for i, (cod, pl) in enumerate(stationary):
                 nc.tensor.matmul_mx(
-                    out=out_ap,
-                    lhsT=columns(cod, c, half).bitcast(FP8X4),
-                    lhsT_scale=columns(pl, c, half),
+                    out=y_bank[c, m0][:, :width],
+                    lhsT=cod.bitcast(FP8X4),
+                    lhsT_scale=pl,
                     rhs=h_cod[:, i, m0 : m0 + width].bitcast(FP8X4),
                     rhs_scale=h_pl[4 * i : P, m0 : m0 + width],
                     start=(i == 0),
                     stop=(i == 3),
                 )
 
-        ybank, yb = {}, {}
+        def copy_y(c, m0, width):
+            nc.scalar.copy(out=y_sb[c // 4][:, c % 4, m0 : m0 + width], in_=y_bank[c, m0][:, :width])
 
-        def stage2_wide(c):
-            ybank[c] = bank("ybank")
-            stage2(c, ybank[c][:], 0, 512, range(4))
-
-        def copy_y(c):
+        def store_y(c, count, m0, width):
             g, t = divmod(c, 4)
-            nc.scalar.copy(out=y_sb[g][:, t, :], in_=ybank[c][:])
+            nc.sync.dma_start(
+                out=o_v[g][:, t : t + count, m0 : m0 + width], in_=y_sb[g][:, t : t + count, m0 : m0 + width]
+            )
 
-        def store_y(c):
-            g, t = divmod(c, 4)
-            nc.sync.dma_start(out=o_v[g][:, t, :], in_=y_sb[g][:, t, :])
-
-        last = {}
-
-        def part_x(c, m0, w):
-            last[c, m0] = bank("last")
-            stage2(c, last[c, m0][:, :w], m0, w, range(2))
-
-        def part_k(c, m0, w):
-            stage2(c, last[c, m0][:, :w], m0, w, range(2, 4))
-
-        def copy_part(c, m0, w):
-            nc.scalar.copy(out=y_sb[c // 4][:, c % 4, m0 : m0 + w], in_=last[c, m0][:, :w])
-
-        def copy_part_v(c, m0, w):
-            nc.vector.tensor_copy(out=y_sb[c // 4][:, c % 4, m0 : m0 + w], in_=last[c, m0][:, :w])
-
-        def store_part(c, m0, w):
-            nc.sync.dma_start(out=o_v[c // 4][:, c % 4, m0 : m0 + w], in_=y_sb[c // 4][:, c % 4, m0 : m0 + w])
-
-        def interleave_y(g, m0, width, engine):
+        def round_y(g, m0, width):
             yb[g, m0] = work.tile([P, 1024], BF16, align_bytes=64, tag="yb", name="yb")
-            copy = nc.scalar.copy if engine == "scalar" else nc.vector.tensor_copy
-            copy(
+            nc.vector.tensor_copy(
                 out=yb[g, m0][:, : 4 * width].rearrange("p (m t) -> p m t", t=4),
                 in_=y_sb[g][:, :, m0 : m0 + width].rearrange("p t m -> p m t"),
             )
@@ -282,164 +269,106 @@ def tile_factoredcubicvolterraequalizer_x2_kernel(
 
         def store_scales(g):
             for q in range(4):
-                eng = nc.sync
-                eng.dma_start(
+                nc.sync.dma_start(
                     out=out_2[g, 4 * q : 4 * q + 4, :].bitcast(I32), in_=y_pl[g][32 * q : 32 * q + 4, :].bitcast(I32)
                 )
 
-        def p_of(d, h):
-            stage1(d, h, a_cod, 0, pb, "pb")
-
-        def q_of(d, h):
-            stage1(d, h, b_cod, 1, qb, "qb")
-
-        def warm_up(count):
-            wb = bank("wb")
-            for i in range(count):
+        def warm_up():
+            idle_bank = bank("idle")
+            for i in range(WARM_UPS):
                 nc.tensor.matmul_mx(
-                    out=wb[:, 0:P],
-                    lhsT=warm_cod[:].bitcast(FP8X4),
-                    lhsT_scale=warm_pl[:],
+                    out=idle_bank[:],
+                    lhsT=warm_cod[:, 0:P].bitcast(FP8X4),
+                    lhsT_scale=warm_pl[:, 0:P],
                     rhs=warm_cod[:].bitcast(FP8X4),
                     rhs_scale=warm_pl[:],
                     start=True,
                     stop=True,
                 )
 
-        warm_up(8)
-        perm_scales(0)
-        transpose_x(0)
-        copy_x(0)
-        transpose_x(1)
-        copy_x(1)
-        quant_x(0)
-        warm_up(8)
-        perm(a_cod, a_raw, 0, 2)
-        transpose_x(2)
-        copy_x(2)
-        perm(a_cod, a_raw, 2, 4)
-        transpose_x(3)
-        copy_x(3)
-        quant_x(1)
-        warm_up(8)
-        perm_scales(1)
-        p_of(0, 0)
-        copy_p(0, 0)
-        perm(b_cod, b_raw, 0, 2)
-        p_of(0, 1)
-        copy_p(0, 1)
-        perm(b_cod, b_raw, 2, 4)
-        p_of(1, 0)
-        copy_p(1, 0)
-        permute_words(0)
-        p_of(1, 1)
-        copy_p(1, 1)
-        q_of(0, 0)
-        make_k2(0, 0)
-        q_of(0, 1)
-        make_k2(0, 1)
-        transpose_x(4)
-        copy_x(4)
-        permute_words(1)
-        transpose_x(5)
-        copy_x(5)
+        deal_scales(0)
+        for c in range(2):
+            transpose_x(c)
+            copy_x(c)
+            quant_x_one(c)
+        warm_up()
+        for h in range(2):
+            deal_words(0, h)
+            p_of(0, h)
+
+        for c in (2, 3):
+            sort_one(c)
+            transpose_x(c)
+            copy_x(c)
+        deal_scales(1)
+        for h in range(2):
+            deal_words(1, h)
+            q_of(0, h)
+        for c in (2, 3):
+            quant_x_one(c)
+        for h in range(2):
+            p_of(1, h)
+
+        for i in range(2):
+            sort_two(i)
+            make_k2(0, i)
+        for c in range(4, TILES):
+            transpose_x(c)
+            copy_x(c)
+        for h in range(2):
+            q_of(1, h)
         make_k3(0)
-        q_of(1, 0)
-        cast_k2(0)
-        quant_x(2)
-        q_of(1, 1)
-        cast_k2(1)
+        quant_x_two(2)
         make_k2(1, 0)
-        transpose_x(6)
-        copy_x(6)
+        quant_x_two(3)
         make_k2(1, 1)
-        transpose_x(7)
-        copy_x(7)
         make_k3(1)
-        p_of(2, 0)
-        copy_p(2, 0)
-        quant_x(3)
-        p_of(2, 1)
-        copy_p(2, 1)
-        quant_k(0)
-        q_of(2, 0)
-        cast_k2(2)
-        make_k2(2, 0)
-        q_of(2, 1)
-        cast_k2(3)
-        make_k2(2, 1)
-        p_of(3, 0)
-        copy_p(3, 0)
-        quant_k(1)
-        p_of(3, 1)
-        copy_p(3, 1)
-        make_k3(2)
-        q_of(3, 0)
-        cast_k2(4)
-        make_k3(3)
-        q_of(3, 1)
-        cast_k2(5)
-        make_k2(3, 0)
-        stage2_wide(0)
-        copy_y(0)
-        make_k2(3, 1)
-        store_y(0)
-        stage2_wide(1)
-        cast_k2(6)
-        quant_k(2)
-        stage2_wide(2)
-        cast_k2(7)
-        quant_k(3)
-        stage2_wide(3)
-        copy_y(1)
-        make_k3(4)
-        store_y(1)
-        copy_y(2)
-        make_k3(5)
-        store_y(2)
-        copy_y(3)
-        quant_k(4)
-        store_y(3)
-        stage2_wide(4)
-        copy_y(4)
-        make_k3(6)
-        store_y(4)
-        quant_k(5)
-        stage2_wide(5)
-        copy_y(5)
-        make_k3(7)
-        part_x(6, 0, 256)
-        quant_k(6)
-        part_k(6, 0, 256)
-        copy_part(6, 0, 256)
-        quant_k(7)
-        part_x(7, 0, 256)
-        interleave_y(0, 0, 256, "vector")
-        part_k(7, 0, 256)
-        copy_part(7, 0, 256)
-        interleave_y(0, 256, 256, "vector")
-        part_x(6, 256, 256)
-        quant_y(0, 0, 256)
-        part_k(6, 256, 256)
-        copy_part(6, 256, 256)
-        quant_y(0, 256, 256)
-        store_codes(0, 0, 512)
-        part_x(7, 256, 128)
-        interleave_y(1, 0, 256, "vector")
+
+        for d in (2, 3):
+            early = 2 * (d - 2)
+            round_k2(early)
+            for h in range(2):
+                p_of(d, h)
+            round_k2(early + 1)
+            for h in range(2):
+                q_of(d, h)
+                make_k2(d, h)
+            for c in (early, early + 1):
+                quant_k(c)
+            if d == 2:
+                make_k3(2)
+                make_k3(3)
+
+        for c in range(0, 4, 2):
+            for s in range(2):
+                round_k2(c + 4 + s)
+                make_k3(c + 4 + s)
+            for s in range(2):
+                quant_k(c + 4 + s)
+                respond(c + s, 0, O)
+                copy_y(c + s, 0, O)
+                store_y(c + s, 1, 0, O)
+        for c in (4, 5):
+            respond(c, 0, O)
+            copy_y(c, 0, O)
+            round_y(0, 256 * (c - 4), 256)
+            store_y(c, 1, 0, O)
+        for m0 in (0, 256):
+            quant_y(0, m0, 256)
+        store_codes(0, 0, O)
         store_scales(0)
-        part_k(7, 256, 128)
-        copy_part(7, 256, 128)
-        interleave_y(1, 256, 128, "vector")
-        store_y(5)
-        part_x(7, 384, 128)
-        quant_y(1, 0, 256)
-        store_part(6, 0, 512)
-        part_k(7, 384, 128)
-        copy_part(7, 384, 128)
-        interleave_y(1, 384, 128, "vector")
-        store_part(7, 0, 512)
-        quant_y(1, 256, 128)
+
+        for i, (m0, width) in enumerate(END_PIECES):
+            for c in (6, 7):
+                respond(c, m0, width)
+                copy_y(c, m0, width)
+            round_y(1, m0, width)
+            if i > 0:
+                quant_y(1, *END_PIECES[i - 1])
+            if i == 0:
+                store_y(6, 2, 0, 256)
         store_codes(1, 0, 256)
-        quant_y(1, 384, 128)
+        store_y(6, 2, 256, 256)
+        quant_y(1, *END_PIECES[-1])
         store_codes(1, 256, 256)
         store_scales(1)

@@ -15,9 +15,7 @@ FLOPS = 2 * T * (N * R * 2 + N * O + R * O * 2)
 P = 128
 TILES = 8
 PAIRS = 4
-SORTED_FROM = 2
-WARM_UPS = 3
-END_PIECES = ((0, 256), (256, 128), (384, 128))
+WARM_UPS = 2
 
 
 def tile_factoredcubicvolterraequalizer_x2_kernel(
@@ -37,18 +35,16 @@ def tile_factoredcubicvolterraequalizer_x2_kernel(
         ident = keep.tile([P, P], F32, align_bytes=64)
         w_pl_raw = kept("w_pl_raw", [P, R], U8, 2)
         w_pl = kept("w_pl", [P, R], U8, 2)
-        w_raw = kept("w_raw", [P, 2, R], I32, 2)
-        w_cod = kept("w_cod", [P, 2, R], I32, 2)
+        w_raw = [kept("w_raw%d_" % i, [P, R], I32, 2) for i in range(2)]
+        w_cod = [kept("w_cod%d_" % i, [P, R], I32, 2) for i in range(2)]
         h_pl = keep.tile([P, O], U8, align_bytes=64)
         h_cod = keep.tile([P, 4, O], I32, align_bytes=64)
-        x_one = kept("x_one", [P, 1, N], BF16, 4)
-        x_two = kept("x_two", [P, 2, N], BF16, 2)
-        x_sorted_one = kept("x_sorted_one", [P, 1, 512], F32, 2)
-        x_sorted_two = kept("x_sorted_two", [P, 2, 512], F32, 2)
-        xb_one = kept("xb_one", [P, 2, P, 4], BF16, 4)
-        xb_two = kept("xb_two", [P, 2, 2 * P, 4], BF16, 2)
-        x_cod = kept("x_cod", [P, 2, 256], I32, PAIRS)
-        x_pl = kept("x_pl", [P, 2, 256], U8, PAIRS)
+        x_first = kept("x_first", [P, 2, 512], BF16, 2)
+        x_raw = kept("x_raw", [P, N], BF16, TILES - 2)
+        x_sorted = kept("x_sorted", [P, 512], F32, TILES - 2)
+        xb = [kept("xb%d_" % d, [P, 2 * P, 4], BF16, 2) for d in range(PAIRS)]
+        x_cod = [kept("x_cod%d_" % d, [P, 256], I32, 2) for d in range(PAIRS)]
+        x_pl = [kept("x_pl%d_" % d, [P, 256], U8, 2) for d in range(PAIRS)]
         p_sb = kept("p_sb", [P, 2, 256, 2], F32, PAIRS)
         k2_sb = kept("k2_sb", [P, 2, 256, 2], F32, PAIRS)
         kb = kept("kb", [P, 2, P, 2, 2], BF16, TILES)
@@ -56,7 +52,7 @@ def tile_factoredcubicvolterraequalizer_x2_kernel(
         k_pl = kept("k_pl", [P, 256], U8, TILES)
         y_sb = kept("y_sb", [P, 4, O], F32, 2)
         y_cod = kept("y_cod", [P, O], I32, 2)
-        y_pl = kept("y_pl", [P, O], U8, 2)
+        y_pl = keep.tile([P, O], U8, align_bytes=64)
         zero = keep.tile([P, 512], BF16, align_bytes=64)
         warm_cod = keep.tile([P, 512], I32, align_bytes=64)
         warm_pl = keep.tile([P, 512], U8, align_bytes=64)
@@ -83,22 +79,22 @@ def tile_factoredcubicvolterraequalizer_x2_kernel(
                     in_=scales[:, 4 * q : 4 * q + 4, :].bitcast(I32),
                 )
 
-        def load_x_one(c):
-            nc.sync.dma_start(out=x_one[c][:], in_=x_v[0][:, c : c + 1, :])
+        def load_x(c):
+            nc.sync.dma_start(out=x_raw[c - 2][:], in_=x_v[c // 4][:, c % 4, :])
 
-        def load_x_two(i):
-            nc.sync.dma_start(out=x_two[i][:], in_=x_v[1][:, 2 * i : 2 * i + 2, :])
+        def load_weight(i, words, scales):
+            load_scales(w_pl_raw[i], 0, scales)
+            for g in range(2):
+                nc.sync.dma_start(out=w_raw[i][g][:], in_=words[g].rearrange("p n t -> p (n t)").bitcast(I32))
 
-        load_x_one(0)
-        load_x_one(1)
-        load_scales(w_pl_raw[0], 0, a_scales)
-        load_words(w_raw[0][:], a_words)
-        load_x_one(2)
-        load_x_one(3)
-        load_scales(w_pl_raw[1], 0, b_scales)
-        load_words(w_raw[1][:], b_words)
-        load_x_two(0)
-        load_x_two(1)
+        for g in range(2):
+            nc.sync.dma_start(out=x_first[g][:], in_=x_v[0][:, 0:2, 512 * g : 512 * (g + 1)])
+        load_weight(0, a_words, a_scales)
+        load_x(2)
+        load_x(3)
+        load_weight(1, b_words, b_scales)
+        for c in range(4, TILES):
+            load_x(c)
         load_words(h_cod[:, 0:2, :], h1_words)
         load_words(h_cod[:, 2:3, :], h2_words)
         load_words(h_cod[:, 3:4, :], h3_words)
@@ -111,61 +107,40 @@ def tile_factoredcubicvolterraequalizer_x2_kernel(
 
         xt, pq_bank, y_bank, yb = {}, {}, {}, {}
 
-        def sort_words(dst, src):
+        def sort_words(c):
             nc.vector.tensor_copy(
-                out=dst[:].rearrange("p s (g u k) -> p (s g) u k", g=2, u=2),
-                in_=src[:].bitcast(F32).rearrange("p s (g k u) -> p (s g) u k", g=2, u=2),
+                out=x_sorted[c - 2][:].rearrange("p (g u k) -> p g u k", g=2, u=2),
+                in_=x_raw[c - 2][:].bitcast(F32).rearrange("p (g k u) -> p g u k", g=2, u=2),
             )
 
-        def sort_one(c):
-            sort_words(x_sorted_one[c - SORTED_FROM], x_one[c])
-
-        def sort_two(i):
-            sort_words(x_sorted_two[i], x_two[i])
-
-        def transpose_x(c):
-            xt[c] = bank("xt")
-            for g in range(2):
+        def transpose_x(d, g):
+            xt[d, g] = bank("xt")
+            for half in range(2):
                 for u in range(2):
-                    col = (2 * g + u) * P
-                    if c < SORTED_FROM:
-                        in_ = x_one[c][:, 0, :].bitcast(F32)[:, 256 * g + u : 256 * (g + 1) : 2]
-                    elif c < 4:
-                        in_ = x_sorted_one[c - SORTED_FROM][:, 0, col : col + P]
+                    if d == 0:
+                        in_ = x_first[g][:, half, :].bitcast(F32)[:, u::2]
                     else:
-                        in_ = x_sorted_two[(c - 4) // 2][:, c % 2, col : col + P]
-                    nc.tensor.transpose(xt[c][:, col : col + P], in_, ident[:])
+                        in_ = x_sorted[2 * d + half - 2][:, (2 * g + u) * P : (2 * g + u + 1) * P]
+                    col = (2 * half + u) * P
+                    nc.tensor.transpose(xt[d, g][:, col : col + P], in_, ident[:])
 
-        def copy_x(c):
-            if c < 4:
-                dst = xb_one[c][:]
-            else:
-                dst = xb_two[(c - 4) // 2][:, :, (c % 2) * P : (c % 2 + 1) * P, :]
+        def copy_x(d, g):
             nc.scalar.copy(
-                out=dst.rearrange("p g r e -> p g (r e)").bitcast(F32).rearrange("p g (r u) -> p g r u", u=2),
-                in_=xt[c][:].rearrange("p (g u r) -> p g r u", g=2, u=2),
+                out=xb[d][g][:].rearrange("p r e -> p (r e)").bitcast(F32).rearrange("p (s r u) -> p s r u", s=2, u=2),
+                in_=xt[d, g][:].rearrange("p (s u r) -> p s r u", s=2, u=2),
             )
 
-        def quant_x_one(c):
-            d, half = divmod(c, 2)
-            for g in range(2):
-                nc.vector.quantize_mx(
-                    out=x_cod[d][:, g, half * P : (half + 1) * P].bitcast(FP8X4),
-                    scales=x_pl[d][:, g, half * P : (half + 1) * P],
-                    in_=xb_one[c][:, g, :, :].rearrange("p r e -> p (r e)"),
-                )
-
-        def quant_x_two(d):
+        def quant_x(d, g):
             nc.vector.quantize_mx(
-                out=x_cod[d][:].rearrange("p g r -> p (g r)").bitcast(FP8X4),
-                scales=x_pl[d][:].rearrange("p g r -> p (g r)"),
-                in_=xb_two[d - 2][:].rearrange("p g r e -> p (g r e)"),
+                out=x_cod[d][g][:].bitcast(FP8X4),
+                scales=x_pl[d][g][:],
+                in_=xb[d][g][:].rearrange("p r e -> p (r e)"),
             )
 
-        def deal_words(i, h):
+        def deal_words(i, g):
             nc.vector.tensor_copy(
-                out=w_cod[i][:].rearrange("p g (t m) -> p g m t", t=4)[:, :, :, 2 * h : 2 * h + 2],
-                in_=w_raw[i][:].rearrange("p g (m t) -> p g m t", t=4)[:, :, :, 2 * h : 2 * h + 2],
+                out=w_cod[i][g][:].rearrange("p (t m) -> p m t", t=4),
+                in_=w_raw[i][g][:].rearrange("p (m t) -> p m t", t=4),
             )
 
         def deal_scales(i):
@@ -174,27 +149,32 @@ def tile_factoredcubicvolterraequalizer_x2_kernel(
                 in_=w_pl_raw[i][:].rearrange("p (m t) -> p t m", t=4),
             )
 
-        def project(i, d, h):
+        def project_pass(i, d, t, g, start, stop):
+            h, j = divmod(t, 2)
+            nc.tensor.matmul_mx(
+                out=pq_bank[i, d, h][:, j * 256 : (j + 1) * 256],
+                lhsT=w_cod[i][g][:, t * P : (t + 1) * P].bitcast(FP8X4),
+                lhsT_scale=w_pl[i][4 * g : P, t * P : (t + 1) * P],
+                rhs=x_cod[d][g][:].bitcast(FP8X4),
+                rhs_scale=x_pl[d][g][:],
+                start=start,
+                stop=stop,
+            )
+
+        def project_k_half(i, d, g):
+            for t in range(4):
+                if g == 0 and t % 2 == 0:
+                    pq_bank[i, d, t // 2] = bank("pq")
+                project_pass(i, d, t, g, g == 0 and t % 2 == 0, g == 1 and t % 2 == 1)
+
+        def project_bank(i, d, h):
             pq_bank[i, d, h] = bank("pq")
-            for j in range(2):
-                t = 2 * h + j
+            for t in (2 * h, 2 * h + 1):
                 for g in range(2):
-                    nc.tensor.matmul_mx(
-                        out=pq_bank[i, d, h][:, j * 256 : (j + 1) * 256],
-                        lhsT=w_cod[i][:, g, t * P : (t + 1) * P].bitcast(FP8X4),
-                        lhsT_scale=w_pl[i][4 * g : P, t * P : (t + 1) * P],
-                        rhs=x_cod[d][:, g, :].bitcast(FP8X4),
-                        rhs_scale=x_pl[d][:, g, :],
-                        start=(g == 0),
-                        stop=(g == 1),
-                    )
+                    project_pass(i, d, t, g, g == 0, g == 1)
 
-        def p_of(d, h):
-            project(0, d, h)
+        def copy_p(d, h):
             nc.scalar.copy(out=p_sb[d][:, h, :, :], in_=pq_bank[0, d, h][:].rearrange("p (j n) -> p n j", j=2))
-
-        def q_of(d, h):
-            project(1, d, h)
 
         def make_k2(d, h):
             nc.vector.tensor_tensor(
@@ -221,13 +201,13 @@ def tile_factoredcubicvolterraequalizer_x2_kernel(
                 in_=kb[c][:].rearrange("p i n h j -> p (i n h j)"),
             )
 
-        def respond(c, m0, width):
+        def respond_passes(c, m0, width, passes):
             d, half = divmod(c, 2)
-            y_bank[c, m0] = bank("y")
             stationary = [
-                (x_cod[d][:, g, half * P : (half + 1) * P], x_pl[d][:, g, half * P : (half + 1) * P]) for g in range(2)
+                (x_cod[d][g][:, half * P : (half + 1) * P], x_pl[d][g][:, half * P : (half + 1) * P]) for g in range(2)
             ] + [(k_cod[c][:, i * P : (i + 1) * P], k_pl[c][:, i * P : (i + 1) * P]) for i in range(2)]
-            for i, (cod, pl) in enumerate(stationary):
+            for i in passes:
+                cod, pl = stationary[i]
                 nc.tensor.matmul_mx(
                     out=y_bank[c, m0][:, :width],
                     lhsT=cod.bitcast(FP8X4),
@@ -237,6 +217,17 @@ def tile_factoredcubicvolterraequalizer_x2_kernel(
                     start=(i == 0),
                     stop=(i == 3),
                 )
+
+        def respond_linear(c, m0, width):
+            y_bank[c, m0] = bank("y")
+            respond_passes(c, m0, width, (0, 1))
+
+        def respond_cubic(c, m0, width):
+            respond_passes(c, m0, width, (2, 3))
+
+        def respond(c, m0, width):
+            respond_linear(c, m0, width)
+            respond_cubic(c, m0, width)
 
         def copy_y(c, m0, width):
             nc.scalar.copy(out=y_sb[c // 4][:, c % 4, m0 : m0 + width], in_=y_bank[c, m0][:, :width])
@@ -257,7 +248,7 @@ def tile_factoredcubicvolterraequalizer_x2_kernel(
         def quant_y(g, m0, width):
             nc.vector.quantize_mx(
                 out=y_cod[g][:, m0 : m0 + width].bitcast(FP8X4),
-                scales=y_pl[g][:, m0 : m0 + width],
+                scales=y_pl[4 * g : P, m0 : m0 + width],
                 in_=yb[g, m0][:, : 4 * width],
             )
 
@@ -267,10 +258,11 @@ def tile_factoredcubicvolterraequalizer_x2_kernel(
                 in_=y_cod[g][:, m0 : m0 + width],
             )
 
-        def store_scales(g):
+        def store_scales():
             for q in range(4):
-                nc.sync.dma_start(
-                    out=out_2[g, 4 * q : 4 * q + 4, :].bitcast(I32), in_=y_pl[g][32 * q : 32 * q + 4, :].bitcast(I32)
+                queue = nc.sync if q % 2 else nc.scalar
+                queue.dma_start(
+                    out=out_2[:, 4 * q : 4 * q + 4, :].bitcast(I32), in_=y_pl[32 * q : 32 * q + 8, :].bitcast(I32)
                 )
 
         def warm_up():
@@ -287,51 +279,61 @@ def tile_factoredcubicvolterraequalizer_x2_kernel(
                 )
 
         deal_scales(0)
-        for c in range(2):
-            transpose_x(c)
-            copy_x(c)
-            quant_x_one(c)
+        for g in range(2):
+            transpose_x(0, g)
+            copy_x(0, g)
         warm_up()
-        for h in range(2):
-            deal_words(0, h)
-            p_of(0, h)
+        for g in range(2):
+            deal_words(0, g)
+            quant_x(0, g)
+            project_k_half(0, 0, g)
+        copy_p(0, 0)
 
-        for c in (2, 3):
-            sort_one(c)
-            transpose_x(c)
-            copy_x(c)
+        sort_words(2)
+        sort_words(3)
         deal_scales(1)
-        for h in range(2):
-            deal_words(1, h)
-            q_of(0, h)
-        for c in (2, 3):
-            quant_x_one(c)
-        for h in range(2):
-            p_of(1, h)
+        for g in range(2):
+            transpose_x(1, g)
+            copy_x(1, g)
+        for g in range(2):
+            deal_words(1, g)
+            project_k_half(1, 0, g)
+        copy_p(0, 1)
+        for g in range(2):
+            quant_x(1, g)
+            sort_words(4 + g)
+            project_k_half(0, 1, g)
+        copy_p(1, 0)
 
-        for i in range(2):
-            sort_two(i)
-            make_k2(0, i)
-        for c in range(4, TILES):
-            transpose_x(c)
-            copy_x(c)
+        sort_words(6)
+        make_k2(0, 0)
+        sort_words(7)
+        make_k2(0, 1)
+        for d in (2, 3):
+            for g in range(2):
+                transpose_x(d, g)
+                copy_x(d, g)
+            if d == 2:
+                copy_p(1, 1)
         for h in range(2):
-            q_of(1, h)
+            project_bank(1, 1, h)
+        quant_x(2, 0)
         make_k3(0)
-        quant_x_two(2)
-        make_k2(1, 0)
-        quant_x_two(3)
-        make_k2(1, 1)
+        quant_x(2, 1)
+        for h in range(2):
+            make_k2(1, h)
+            quant_x(3, h)
         make_k3(1)
 
         for d in (2, 3):
             early = 2 * (d - 2)
             round_k2(early)
             for h in range(2):
-                p_of(d, h)
+                project_bank(0, d, h)
+                copy_p(d, h)
             round_k2(early + 1)
             for h in range(2):
-                q_of(d, h)
+                project_bank(1, d, h)
                 make_k2(d, h)
             for c in (early, early + 1):
                 quant_k(c)
@@ -348,27 +350,33 @@ def tile_factoredcubicvolterraequalizer_x2_kernel(
                 respond(c + s, 0, O)
                 copy_y(c + s, 0, O)
                 store_y(c + s, 1, 0, O)
-        for c in (4, 5):
-            respond(c, 0, O)
-            copy_y(c, 0, O)
-            round_y(0, 256 * (c - 4), 256)
-            store_y(c, 1, 0, O)
+
+        for c in range(4, TILES):
+            respond_linear(c, 0, 256)
+        for c in range(4, TILES):
+            respond_cubic(c, 0, 256)
+            copy_y(c, 0, 256)
+            if c % 2:
+                store_y(c - 1, 2, 0, 256)
+        for m0 in (0, 256):
+            round_y(0, m0, 256)
         for m0 in (0, 256):
             quant_y(0, m0, 256)
         store_codes(0, 0, O)
-        store_scales(0)
-
-        for i, (m0, width) in enumerate(END_PIECES):
-            for c in (6, 7):
-                respond(c, m0, width)
-                copy_y(c, m0, width)
-            round_y(1, m0, width)
-            if i > 0:
-                quant_y(1, *END_PIECES[i - 1])
-            if i == 0:
-                store_y(6, 2, 0, 256)
+        round_y(1, 0, 256)
+        quant_y(1, 0, 256)
+        for c in range(4, TILES - 1):
+            respond(c, 256, 256)
+            copy_y(c, 256, 256)
+            if c == 5:
+                store_y(4, 2, 256, 256)
         store_codes(1, 0, 256)
+        for m0 in (256, 384):
+            respond(7, m0, P)
+            copy_y(7, m0, P)
+            round_y(1, m0, P)
         store_y(6, 2, 256, 256)
-        quant_y(1, *END_PIECES[-1])
+        for m0 in (256, 384):
+            quant_y(1, m0, P)
         store_codes(1, 256, 256)
-        store_scales(1)
+        store_scales()

@@ -15,7 +15,6 @@ FLOPS = 2 * T * (N * R * 2 + N * O + R * O * 2)
 P = 128
 TILES = 8
 PAIRS = 4
-WARM_UPS = 2
 
 
 def tile_factoredcubicvolterraequalizer_x2_kernel(
@@ -50,21 +49,23 @@ def tile_factoredcubicvolterraequalizer_x2_kernel(
         kb = kept("kb", [P, 2, P, 2, 2], BF16, TILES)
         k_cod = kept("k_cod", [P, 256], I32, TILES)
         k_pl = kept("k_pl", [P, 256], U8, TILES)
-        y_sb = kept("y_sb", [P, 4, O], F32, 2)
+        y_first = keep.tile([P, 4, O], F32, align_bytes=64)
+        y_second = kept("y_second", [P, 4, 256], F32, 2)
         y_cod = kept("y_cod", [P, O], I32, 2)
         y_pl = keep.tile([P, O], U8, align_bytes=64)
-        zero = keep.tile([P, 512], BF16, align_bytes=64)
+        zero = keep.tile([P, P], BF16, align_bytes=64)
         warm_cod = keep.tile([P, 512], I32, align_bytes=64)
         warm_pl = keep.tile([P, 512], U8, align_bytes=64)
 
         x_v = [x[512 * g : 512 * g + 512, :].rearrange("(p t) k -> p t k", t=4) for g in range(2)]
         o_v = [out_0[512 * g : 512 * g + 512, :].rearrange("(p t) m -> p t m", t=4) for g in range(2)]
 
-        for plane in (w_pl_raw[0], w_pl_raw[1], h_pl, warm_pl):
-            nc.vector.memset(plane[:].bitcast(I32), 0)
         nc.vector.memset(zero[:].bitcast(I32), 0)
-        nc.vector.memset(warm_cod[:], 0)
-        nc.vector.quantize_mx(out=warm_cod[:, 0:P].bitcast(FP8X4), scales=warm_pl[:, 0:P], in_=zero[:])
+        nc.vector.memset(warm_cod[:, 32:], 0)
+        nc.vector.memset(warm_pl[:].bitcast(I32), 0)
+        nc.vector.quantize_mx(out=warm_cod[:, 0:32].bitcast(FP8X4), scales=warm_pl[:, 0:32], in_=zero[:])
+        for plane in (w_pl_raw[0], w_pl_raw[1], h_pl):
+            nc.vector.memset(plane[:].bitcast(I32), 0)
         make_identity(nc, ident[:])
 
         def load_words(tile_ap, words):
@@ -109,8 +110,8 @@ def tile_factoredcubicvolterraequalizer_x2_kernel(
 
         def sort_words(c):
             nc.vector.tensor_copy(
-                out=x_sorted[c - 2][:].rearrange("p (g u k) -> p g u k", g=2, u=2),
-                in_=x_raw[c - 2][:].bitcast(F32).rearrange("p (g k u) -> p g u k", g=2, u=2),
+                out=x_sorted[c - 2][:].rearrange("p (g u k e) -> p g k u e", g=2, u=2, e=2),
+                in_=x_raw[c - 2][:].bitcast(F32).rearrange("p (g k e u) -> p g k u e", g=2, u=2, e=2),
             )
 
         def transpose_x(d, g):
@@ -139,8 +140,8 @@ def tile_factoredcubicvolterraequalizer_x2_kernel(
 
         def deal_words(i, g):
             nc.vector.tensor_copy(
-                out=w_cod[i][g][:].rearrange("p (t m) -> p m t", t=4),
-                in_=w_raw[i][g][:].rearrange("p (m t) -> p m t", t=4),
+                out=w_cod[i][g][:].rearrange("p (t m e) -> p m t e", t=4, e=2),
+                in_=w_raw[i][g][:].rearrange("p (m e t) -> p m t e", t=4, e=2),
             )
 
         def deal_scales(i):
@@ -229,20 +230,26 @@ def tile_factoredcubicvolterraequalizer_x2_kernel(
             respond_linear(c, m0, width)
             respond_cubic(c, m0, width)
 
+        def y_sb(g, t0, t1, m0, width):
+            if g == 0:
+                return y_first[:, t0:t1, m0 : m0 + width]
+            return y_second[m0 // 256][:, t0:t1, m0 % 256 : m0 % 256 + width]
+
         def copy_y(c, m0, width):
-            nc.scalar.copy(out=y_sb[c // 4][:, c % 4, m0 : m0 + width], in_=y_bank[c, m0][:, :width])
+            g, t = divmod(c, 4)
+            nc.scalar.copy(out=y_sb(g, t, t + 1, m0, width), in_=y_bank[c, m0][:, :width].rearrange("p (o m) -> p o m", o=1))
 
         def store_y(c, count, m0, width):
             g, t = divmod(c, 4)
             nc.sync.dma_start(
-                out=o_v[g][:, t : t + count, m0 : m0 + width], in_=y_sb[g][:, t : t + count, m0 : m0 + width]
+                out=o_v[g][:, t : t + count, m0 : m0 + width], in_=y_sb(g, t, t + count, m0, width)
             )
 
-        def round_y(g, m0, width):
+        def round_y(g, m0, width, run=2):
             yb[g, m0] = work.tile([P, 1024], BF16, align_bytes=64, tag="yb", name="yb")
             nc.vector.tensor_copy(
-                out=yb[g, m0][:, : 4 * width].rearrange("p (m t) -> p m t", t=4),
-                in_=y_sb[g][:, :, m0 : m0 + width].rearrange("p t m -> p m t"),
+                out=yb[g, m0][:, : 4 * width].rearrange("p (m e t) -> p m t e", t=4, e=run),
+                in_=y_sb(g, 0, 4, m0, width).rearrange("p t (m e) -> p m t e", e=run),
             )
 
         def quant_y(g, m0, width):
@@ -265,9 +272,9 @@ def tile_factoredcubicvolterraequalizer_x2_kernel(
                     out=out_2[:, 4 * q : 4 * q + 4, :].bitcast(I32), in_=y_pl[32 * q : 32 * q + 8, :].bitcast(I32)
                 )
 
-        def warm_up():
+        def warm_up(count):
             idle_bank = bank("idle")
-            for i in range(WARM_UPS):
+            for i in range(count):
                 nc.tensor.matmul_mx(
                     out=idle_bank[:],
                     lhsT=warm_cod[:, 0:P].bitcast(FP8X4),
@@ -278,11 +285,12 @@ def tile_factoredcubicvolterraequalizer_x2_kernel(
                     stop=True,
                 )
 
+        warm_up(2)
         deal_scales(0)
         for g in range(2):
             transpose_x(0, g)
             copy_x(0, g)
-        warm_up()
+        warm_up(2)
         for g in range(2):
             deal_words(0, g)
             quant_x(0, g)
@@ -374,7 +382,7 @@ def tile_factoredcubicvolterraequalizer_x2_kernel(
         for m0 in (256, 384):
             respond(7, m0, P)
             copy_y(7, m0, P)
-            round_y(1, m0, P)
+            round_y(1, m0, P, 1)
         store_y(6, 2, 256, 256)
         for m0 in (256, 384):
             quant_y(1, m0, P)

@@ -35,7 +35,7 @@ def tile_factoredcubicvolterraequalizer_x2_kernel(
         w_pl_raw = kept("w_pl_raw", [P, R], U8, 2)
         w_pl = kept("w_pl", [P, R], U8, 2)
         w_raw = [kept("w_raw%d_" % i, [P, R], I32, 2) for i in range(2)]
-        w_cod = [kept("w_cod%d_" % i, [P, R], I32, 2) for i in range(2)]
+        w_cod = [[kept("w_cod%d_%d_" % (i, g), [P, 2 * P], I32, 2) for g in range(2)] for i in range(2)]
         h_pl = keep.tile([P, O], U8, align_bytes=64)
         h_cod = keep.tile([P, 4, O], I32, align_bytes=64)
         x_first = kept("x_first", [P, 2, 512], BF16, 2)
@@ -138,10 +138,10 @@ def tile_factoredcubicvolterraequalizer_x2_kernel(
                 in_=xb[d][g][:].rearrange("p r e -> p (r e)"),
             )
 
-        def deal_words(i, g):
+        def deal_words(i, g, h):
             nc.vector.tensor_copy(
-                out=w_cod[i][g][:].rearrange("p (t m e) -> p m t e", t=4, e=2),
-                in_=w_raw[i][g][:].rearrange("p (m e t) -> p m t e", t=4, e=2),
+                out=w_cod[i][g][h][:].rearrange("p (j m) -> p m j", j=2),
+                in_=w_raw[i][g][:].rearrange("p (m t) -> p m t", t=4)[:, :, 2 * h : 2 * h + 2],
             )
 
         def deal_scales(i):
@@ -154,7 +154,7 @@ def tile_factoredcubicvolterraequalizer_x2_kernel(
             h, j = divmod(t, 2)
             nc.tensor.matmul_mx(
                 out=pq_bank[i, d, h][:, j * 256 : (j + 1) * 256],
-                lhsT=w_cod[i][g][:, t * P : (t + 1) * P].bitcast(FP8X4),
+                lhsT=w_cod[i][g][h][:, j * P : (j + 1) * P].bitcast(FP8X4),
                 lhsT_scale=w_pl[i][4 * g : P, t * P : (t + 1) * P],
                 rhs=x_cod[d][g][:].bitcast(FP8X4),
                 rhs_scale=x_pl[d][g][:],
@@ -245,11 +245,11 @@ def tile_factoredcubicvolterraequalizer_x2_kernel(
                 out=o_v[g][:, t : t + count, m0 : m0 + width], in_=y_sb(g, t, t + count, m0, width)
             )
 
-        def round_y(g, m0, width, run=2):
+        def round_y(g, m0, width):
             yb[g, m0] = work.tile([P, 1024], BF16, align_bytes=64, tag="yb", name="yb")
             nc.vector.tensor_copy(
-                out=yb[g, m0][:, : 4 * width].rearrange("p (m e t) -> p m t e", t=4, e=run),
-                in_=y_sb(g, 0, 4, m0, width).rearrange("p t (m e) -> p m t e", e=run),
+                out=yb[g, m0][:, : 4 * width].rearrange("p (m e t) -> p m t e", t=4, e=2),
+                in_=y_sb(g, 0, 4, m0, width).rearrange("p t (m e) -> p m t e", e=2),
             )
 
         def quant_y(g, m0, width):
@@ -292,8 +292,9 @@ def tile_factoredcubicvolterraequalizer_x2_kernel(
             copy_x(0, g)
         warm_up(2)
         for g in range(2):
-            deal_words(0, g)
+            deal_words(0, g, 0)
             quant_x(0, g)
+            deal_words(0, g, 1)
             project_k_half(0, 0, g)
         copy_p(0, 0)
 
@@ -304,7 +305,8 @@ def tile_factoredcubicvolterraequalizer_x2_kernel(
             transpose_x(1, g)
             copy_x(1, g)
         for g in range(2):
-            deal_words(1, g)
+            for h in range(2):
+                deal_words(1, g, h)
             project_k_half(1, 0, g)
         copy_p(0, 1)
         for g in range(2):
@@ -313,8 +315,8 @@ def tile_factoredcubicvolterraequalizer_x2_kernel(
             project_k_half(0, 1, g)
         copy_p(1, 0)
 
-        sort_words(6)
         make_k2(0, 0)
+        sort_words(6)
         sort_words(7)
         make_k2(0, 1)
         for d in (2, 3):
@@ -325,9 +327,9 @@ def tile_factoredcubicvolterraequalizer_x2_kernel(
                 copy_p(1, 1)
         for h in range(2):
             project_bank(1, 1, h)
-        quant_x(2, 0)
         make_k3(0)
-        quant_x(2, 1)
+        for g in range(2):
+            quant_x(2, g)
         for h in range(2):
             make_k2(1, h)
             quant_x(3, h)
@@ -382,7 +384,7 @@ def tile_factoredcubicvolterraequalizer_x2_kernel(
         for m0 in (256, 384):
             respond(7, m0, P)
             copy_y(7, m0, P)
-            round_y(1, m0, P, 1)
+            round_y(1, m0, P)
         store_y(6, 2, 256, 256)
         for m0 in (256, 384):
             quant_y(1, m0, P)

@@ -83,17 +83,18 @@ def tile_factoredcubicvolterraequalizer_x2_kernel(
         def load_x(c):
             nc.sync.dma_start(out=x_raw[c - 2][:], in_=x_v[c // 4][:, c % 4, :])
 
-        def load_weight(i, words, scales):
-            load_scales(w_pl_raw[i], 0, scales)
+        def load_weight(i, words):
             for g in range(2):
                 nc.sync.dma_start(out=w_raw[i][g][:], in_=words[g].rearrange("p n t -> p (n t)").bitcast(I32))
 
         for g in range(2):
             nc.sync.dma_start(out=x_first[g][:], in_=x_v[0][:, 0:2, 512 * g : 512 * (g + 1)])
-        load_weight(0, a_words, a_scales)
         load_x(2)
         load_x(3)
-        load_weight(1, b_words, b_scales)
+        load_scales(w_pl_raw[0], 0, a_scales)
+        load_weight(0, a_words)
+        load_weight(1, b_words)
+        load_scales(w_pl_raw[1], 0, b_scales)
         for c in range(4, TILES):
             load_x(c)
         load_words(h_cod[:, 0:2, :], h1_words)
@@ -108,22 +109,27 @@ def tile_factoredcubicvolterraequalizer_x2_kernel(
 
         xt, pq_bank, y_bank, yb = {}, {}, {}, {}
 
-        def sort_words(c):
-            nc.vector.tensor_copy(
+        def sort_words(c, copy=nc.vector.tensor_copy):
+            copy(
                 out=x_sorted[c - 2][:].rearrange("p (g u k e) -> p g k u e", g=2, u=2, e=2),
                 in_=x_raw[c - 2][:].bitcast(F32).rearrange("p (g k e u) -> p g k u e", g=2, u=2, e=2),
             )
 
-        def transpose_x(d, g):
-            xt[d, g] = bank("xt")
+        def transpose_x(d, g, half):
+            if half == 0:
+                xt[d, g] = bank("xt")
+            for u in range(2):
+                if d == 0:
+                    in_ = x_first[g][:, half, :].bitcast(F32)[:, u::2]
+                else:
+                    in_ = x_sorted[2 * d + half - 2][:, (2 * g + u) * P : (2 * g + u + 1) * P]
+                col = (2 * half + u) * P
+                nc.tensor.transpose(xt[d, g][:, col : col + P], in_, ident[:])
+
+        def turn_x(d, g):
             for half in range(2):
-                for u in range(2):
-                    if d == 0:
-                        in_ = x_first[g][:, half, :].bitcast(F32)[:, u::2]
-                    else:
-                        in_ = x_sorted[2 * d + half - 2][:, (2 * g + u) * P : (2 * g + u + 1) * P]
-                    col = (2 * half + u) * P
-                    nc.tensor.transpose(xt[d, g][:, col : col + P], in_, ident[:])
+                transpose_x(d, g, half)
+            copy_x(d, g)
 
         def copy_x(d, g):
             nc.scalar.copy(
@@ -285,51 +291,55 @@ def tile_factoredcubicvolterraequalizer_x2_kernel(
                     stop=True,
                 )
 
-        warm_up(2)
-        deal_scales(0)
+        warm_up(3)
         for g in range(2):
-            transpose_x(0, g)
-            copy_x(0, g)
-        warm_up(2)
-        for g in range(2):
-            deal_words(0, g, 0)
-            quant_x(0, g)
-            deal_words(0, g, 1)
-            project_k_half(0, 0, g)
-        copy_p(0, 0)
-
+            turn_x(0, g)
+        warm_up(1)
         sort_words(2)
         sort_words(3)
-        deal_scales(1)
+        for half in range(2):
+            for g in range(2):
+                transpose_x(1, g, half)
         for g in range(2):
-            transpose_x(1, g)
             copy_x(1, g)
+        deal_scales(0)
+        quant_x(0, 0)
         for g in range(2):
             for h in range(2):
-                deal_words(1, g, h)
-            project_k_half(1, 0, g)
-        copy_p(0, 1)
+                deal_words(0, g, h)
+            if g == 0:
+                quant_x(0, 1)
+            project_k_half(0, 0, g)
         for g in range(2):
+            copy_p(0, g)
             quant_x(1, g)
-            sort_words(4 + g)
             project_k_half(0, 1, g)
-        copy_p(1, 0)
+            deal_words(1, g, 0)
+            if g == 1:
+                deal_scales(1)
+            deal_words(1, g, 1)
+        for h in range(2):
+            copy_p(1, h)
+            project_bank(1, 0, h)
 
+        sort_words(4)
+        sort_words(5)
         make_k2(0, 0)
         sort_words(6)
         sort_words(7)
         make_k2(0, 1)
-        for d in (2, 3):
+        for g in range(2):
+            turn_x(2, g)
+        for half in range(2):
             for g in range(2):
-                transpose_x(d, g)
-                copy_x(d, g)
-            if d == 2:
-                copy_p(1, 1)
+                transpose_x(3, g, half)
+        for g in range(2):
+            copy_x(3, g)
         for h in range(2):
             project_bank(1, 1, h)
-        make_k3(0)
         for g in range(2):
             quant_x(2, g)
+        make_k3(0)
         for h in range(2):
             make_k2(1, h)
             quant_x(3, h)
@@ -338,8 +348,12 @@ def tile_factoredcubicvolterraequalizer_x2_kernel(
         for d in (2, 3):
             early = 2 * (d - 2)
             round_k2(early)
+            if d == 2:
+                for g in range(2):
+                    project_k_half(0, d, g)
             for h in range(2):
-                project_bank(0, d, h)
+                if d == 3:
+                    project_bank(0, d, h)
                 copy_p(d, h)
             round_k2(early + 1)
             for h in range(2):

@@ -83,18 +83,19 @@ def tile_factoredcubicvolterraequalizer_x2_kernel(
         def load_x(c):
             nc.sync.dma_start(out=x_raw[c - 2][:], in_=x_v[c // 4][:, c % 4, :])
 
-        def load_weight(i, words):
-            for g in range(2):
-                nc.sync.dma_start(out=w_raw[i][g][:], in_=words[g].rearrange("p n t -> p (n t)").bitcast(I32))
+        def load_weight(i, words, g):
+            nc.sync.dma_start(out=w_raw[i][g][:], in_=words[g].rearrange("p n t -> p (n t)").bitcast(I32))
 
         for g in range(2):
             nc.sync.dma_start(out=x_first[g][:], in_=x_v[0][:, 0:2, 512 * g : 512 * (g + 1)])
         load_x(2)
         load_x(3)
         load_scales(w_pl_raw[0], 0, a_scales)
-        load_weight(0, a_words)
-        load_weight(1, b_words)
+        for g in range(2):
+            load_weight(0, a_words, g)
+        load_weight(1, b_words, 0)
         load_scales(w_pl_raw[1], 0, b_scales)
+        load_weight(1, b_words, 1)
         for c in range(4, TILES):
             load_x(c)
         load_words(h_cod[:, 0:2, :], h1_words)
@@ -314,11 +315,11 @@ def tile_factoredcubicvolterraequalizer_x2_kernel(
             copy_p(0, g)
             quant_x(1, g)
             project_k_half(0, 1, g)
-            deal_words(1, g, 0)
-            if g == 1:
-                deal_scales(1)
-            deal_words(1, g, 1)
         for h in range(2):
+            for g in range(2):
+                deal_words(1, g, h)
+                if g == 0 and h == 0:
+                    deal_scales(1)
             copy_p(1, h)
             project_bank(1, 0, h)
 

@@ -39,8 +39,9 @@ def tile_factoredcubicvolterraequalizer_x2_kernel(
         h_pl = keep.tile([P, O], U8, align_bytes=64)
         h_cod = keep.tile([P, 4, O], I32, align_bytes=64)
         x_first = kept("x_first", [P, 2, 512], BF16, 2)
-        x_raw = kept("x_raw", [P, N], BF16, TILES - 2)
-        x_sorted = kept("x_sorted", [P, 512], F32, TILES - 2)
+        x_pair = kept("x_pair", [P, 2 * N], BF16, 2)
+        x_last = kept("x_last", [P, N], BF16, 2)
+        x_sorted = kept("x_sorted", [P, 512], F32, TILES // 2)
         xb = [kept("xb%d_" % d, [P, 2 * P, 4], BF16, 2) for d in range(PAIRS)]
         x_cod = [kept("x_cod%d_" % d, [P, 256], I32, 2) for d in range(PAIRS)]
         x_pl = [kept("x_pl%d_" % d, [P, 256], U8, 2) for d in range(PAIRS)]
@@ -80,24 +81,25 @@ def tile_factoredcubicvolterraequalizer_x2_kernel(
                     in_=scales[:, 4 * q : 4 * q + 4, :].bitcast(I32),
                 )
 
-        def load_x(c):
-            nc.sync.dma_start(out=x_raw[c - 2][:], in_=x_v[c // 4][:, c % 4, :])
+        def load_pair(d):
+            t0 = 2 * (d % 2)
+            nc.sync.dma_start(out=x_pair[d - 1][:], in_=x_v[d // 2][:, t0 : t0 + 2, :].rearrange("p t k -> p (t k)"))
 
         def load_weight(i, words, g):
             nc.sync.dma_start(out=w_raw[i][g][:], in_=words[g].rearrange("p n t -> p (n t)").bitcast(I32))
 
         for g in range(2):
             nc.sync.dma_start(out=x_first[g][:], in_=x_v[0][:, 0:2, 512 * g : 512 * (g + 1)])
-        load_x(2)
-        load_x(3)
+        load_pair(1)
         load_scales(w_pl_raw[0], 0, a_scales)
         for g in range(2):
             load_weight(0, a_words, g)
         load_weight(1, b_words, 0)
         load_scales(w_pl_raw[1], 0, b_scales)
         load_weight(1, b_words, 1)
-        for c in range(4, TILES):
-            load_x(c)
+        load_pair(2)
+        for half in range(2):
+            nc.sync.dma_start(out=x_last[half][:], in_=x_v[1][:, 2 + half, :])
         load_words(h_cod[:, 0:2, :], h1_words)
         load_words(h_cod[:, 2:3, :], h2_words)
         load_words(h_cod[:, 3:4, :], h3_words)
@@ -110,10 +112,16 @@ def tile_factoredcubicvolterraequalizer_x2_kernel(
 
         xt, pq_bank, y_bank, yb = {}, {}, {}, {}
 
+        def x_words(c):
+            d, half = divmod(c, 2)
+            if d == PAIRS - 1:
+                return x_last[half][:].bitcast(F32)
+            return x_pair[d - 1][:].bitcast(F32)[:, 512 * half : 512 * (half + 1)]
+
         def sort_words(c, copy=nc.vector.tensor_copy):
             copy(
-                out=x_sorted[c - 2][:].rearrange("p (g u k e) -> p g k u e", g=2, u=2, e=2),
-                in_=x_raw[c - 2][:].bitcast(F32).rearrange("p (g k e u) -> p g k u e", g=2, u=2, e=2),
+                out=x_sorted[c - 4][:].rearrange("p (g u k e) -> p g k u e", g=2, u=2, e=2),
+                in_=x_words(c).rearrange("p (g k e u) -> p g k u e", g=2, u=2, e=2),
             )
 
         def transpose_x(d, g, half):
@@ -122,8 +130,10 @@ def tile_factoredcubicvolterraequalizer_x2_kernel(
             for u in range(2):
                 if d == 0:
                     in_ = x_first[g][:, half, :].bitcast(F32)[:, u::2]
+                elif d == 1:
+                    in_ = x_words(2 * d + half)[:, 256 * g + u : 256 * (g + 1) : 2]
                 else:
-                    in_ = x_sorted[2 * d + half - 2][:, (2 * g + u) * P : (2 * g + u + 1) * P]
+                    in_ = x_sorted[2 * d + half - 4][:, (2 * g + u) * P : (2 * g + u + 1) * P]
                 col = (2 * half + u) * P
                 nc.tensor.transpose(xt[d, g][:, col : col + P], in_, ident[:])
 
@@ -292,17 +302,13 @@ def tile_factoredcubicvolterraequalizer_x2_kernel(
                     stop=True,
                 )
 
-        warm_up(3)
+        warm_up(2)
         for g in range(2):
             turn_x(0, g)
         warm_up(1)
-        sort_words(2)
-        sort_words(3)
-        for half in range(2):
-            for g in range(2):
-                transpose_x(1, g, half)
         for g in range(2):
-            copy_x(1, g)
+            turn_x(1, g)
+        warm_up(1)
         deal_scales(0)
         quant_x(0, 0)
         for g in range(2):
@@ -316,19 +322,21 @@ def tile_factoredcubicvolterraequalizer_x2_kernel(
             quant_x(1, g)
             project_k_half(0, 1, g)
         for h in range(2):
-            for g in range(2):
-                deal_words(1, g, h)
-                if g == 0 and h == 0:
-                    deal_scales(1)
+            deal_words(1, 0, h)
+        deal_scales(1)
+        for h in range(2):
+            deal_words(1, 1, h)
             copy_p(1, h)
             project_bank(1, 0, h)
+        project_bank(1, 1, 0)
 
         sort_words(4)
-        sort_words(5)
+        sort_words(5, nc.scalar.copy)
+        sort_words(6, nc.scalar.copy)
         make_k2(0, 0)
-        sort_words(6)
-        sort_words(7)
         make_k2(0, 1)
+        sort_words(7)
+        make_k2(1, 0)
         for g in range(2):
             turn_x(2, g)
         for half in range(2):
@@ -336,14 +344,13 @@ def tile_factoredcubicvolterraequalizer_x2_kernel(
                 transpose_x(3, g, half)
         for g in range(2):
             copy_x(3, g)
-        for h in range(2):
-            project_bank(1, 1, h)
+        project_bank(1, 1, 1)
         for g in range(2):
             quant_x(2, g)
+        make_k2(1, 1)
+        for g in range(2):
+            quant_x(3, g)
         make_k3(0)
-        for h in range(2):
-            make_k2(1, h)
-            quant_x(3, h)
         make_k3(1)
 
         for d in (2, 3):

@@ -24,7 +24,6 @@ def tile_factoredcubicvolterraequalizer_x2_kernel(
     nc = tc.nc
     with ExitStack() as ctx:
         keep = ctx.enter_context(tc.tile_pool(name="keep", bufs=1))
-        work = ctx.enter_context(tc.tile_pool(name="work", bufs=4))
         psum = ctx.enter_context(tc.psum_pool(name="psum", bufs=8))
         ctx.enter_context(tc.manual_schedule())
 
@@ -47,11 +46,12 @@ def tile_factoredcubicvolterraequalizer_x2_kernel(
         x_pl = [kept("x_pl%d_" % d, [P, 256], U8, 2) for d in range(PAIRS)]
         p_sb = kept("p_sb", [P, 2, 256, 2], F32, PAIRS)
         k2_sb = kept("k2_sb", [P, 2, 256, 2], F32, PAIRS)
-        kb = kept("kb", [P, 2, P, 2, 2], BF16, TILES)
-        k_cod = kept("k_cod", [P, 256], I32, TILES)
-        k_pl = kept("k_pl", [P, 256], U8, TILES)
+        kb = kept("kb", [P, 2, 2, P, 2, 2], BF16, PAIRS)
+        k_cod = kept("k_cod", [P, 2, 256], I32, PAIRS)
+        k_pl = kept("k_pl", [P, 2, 256], U8, PAIRS)
         y_first = keep.tile([P, 4, O], F32, align_bytes=64)
         y_second = kept("y_second", [P, 4, 256], F32, 2)
+        yb = kept("yb", [P, 4 * O], BF16, 2)
         y_cod = kept("y_cod", [P, O], I32, 2)
         y_pl = keep.tile([P, O], U8, align_bytes=64)
         zero = keep.tile([P, P], BF16, align_bytes=64)
@@ -110,7 +110,7 @@ def tile_factoredcubicvolterraequalizer_x2_kernel(
         def bank(name):
             return psum.tile([P, 512], F32, tag="bank", name=name)
 
-        xt, pq_bank, y_bank, yb = {}, {}, {}, {}
+        xt, pq_bank, y_bank = {}, {}, {}
 
         def x_words(c):
             d, half = divmod(c, 2)
@@ -202,28 +202,35 @@ def tile_factoredcubicvolterraequalizer_x2_kernel(
                 op=MULT,
             )
 
-        def tokens(tile, c):
+        def tokens(tile, c, count):
             d, half = divmod(c, 2)
-            return tile[d][:, :, half * P : (half + 1) * P, :].rearrange("p h n j -> p n h j")
+            return tile[d][:, :, half * P : (half + count) * P, :].rearrange("p h (s n) j -> p s n h j", s=count)
 
-        def make_k3(c):
-            nc.vector.tensor_tensor(out=kb[c][:, 1, :, :, :], in0=tokens(k2_sb, c), in1=tokens(p_sb, c), op=MULT)
+        def kb_part(c, count, i):
+            d, half = divmod(c, 2)
+            return kb[d][:, half : half + count, i, :, :, :]
 
-        def round_k2(c):
-            nc.scalar.copy(out=kb[c][:, 0, :, :, :], in_=tokens(k2_sb, c))
+        def make_k3(c, count):
+            nc.vector.tensor_tensor(
+                out=kb_part(c, count, 1), in0=tokens(k2_sb, c, count), in1=tokens(p_sb, c, count), op=MULT
+            )
 
-        def quant_k(c):
+        def round_k2(c, count):
+            nc.scalar.copy(out=kb_part(c, count, 0), in_=tokens(k2_sb, c, count))
+
+        def quant_k(c, count):
+            d, half = divmod(c, 2)
             nc.vector.quantize_mx(
-                out=k_cod[c][:].bitcast(FP8X4),
-                scales=k_pl[c][:],
-                in_=kb[c][:].rearrange("p i n h j -> p (i n h j)"),
+                out=k_cod[d][:, half : half + count, :].rearrange("p s w -> p (s w)").bitcast(FP8X4),
+                scales=k_pl[d][:, half : half + count, :].rearrange("p s w -> p (s w)"),
+                in_=kb[d][:, half : half + count, :, :, :, :].rearrange("p s i n h j -> p (s i n h j)"),
             )
 
         def respond_passes(c, m0, width, passes):
             d, half = divmod(c, 2)
             stationary = [
                 (x_cod[d][g][:, half * P : (half + 1) * P], x_pl[d][g][:, half * P : (half + 1) * P]) for g in range(2)
-            ] + [(k_cod[c][:, i * P : (i + 1) * P], k_pl[c][:, i * P : (i + 1) * P]) for i in range(2)]
+            ] + [(k_cod[d][:, half, i * P : (i + 1) * P], k_pl[d][:, half, i * P : (i + 1) * P]) for i in range(2)]
             for i in passes:
                 cod, pl = stationary[i]
                 nc.tensor.matmul_mx(
@@ -262,10 +269,9 @@ def tile_factoredcubicvolterraequalizer_x2_kernel(
                 out=o_v[g][:, t : t + count, m0 : m0 + width], in_=y_sb(g, t, t + count, m0, width)
             )
 
-        def round_y(g, m0, width):
-            yb[g, m0] = work.tile([P, 1024], BF16, align_bytes=64, tag="yb", name="yb")
-            nc.vector.tensor_copy(
-                out=yb[g, m0][:, : 4 * width].rearrange("p (m e t) -> p m t e", t=4, e=2),
+        def round_y(g, m0, width, copy=nc.vector.tensor_copy):
+            copy(
+                out=yb[g][:, 4 * m0 : 4 * (m0 + width)].rearrange("p (m e t) -> p m t e", t=4, e=2),
                 in_=y_sb(g, 0, 4, m0, width).rearrange("p t (m e) -> p m t e", e=2),
             )
 
@@ -273,7 +279,7 @@ def tile_factoredcubicvolterraequalizer_x2_kernel(
             nc.vector.quantize_mx(
                 out=y_cod[g][:, m0 : m0 + width].bitcast(FP8X4),
                 scales=y_pl[4 * g : P, m0 : m0 + width],
-                in_=yb[g, m0][:, : 4 * width],
+                in_=yb[g][:, 4 * m0 : 4 * (m0 + width)],
             )
 
         def store_codes(g, m0, width):
@@ -345,44 +351,54 @@ def tile_factoredcubicvolterraequalizer_x2_kernel(
         for g in range(2):
             copy_x(3, g)
         project_bank(1, 1, 1)
-        for g in range(2):
-            quant_x(2, g)
+        quant_x(2, 0)
+        make_k3(0, 1)
+        quant_x(2, 1)
         make_k2(1, 1)
+        quant_x(3, 0)
+        make_k3(1, 1)
+        quant_x(3, 1)
+        round_k2(0, 2)
         for g in range(2):
-            quant_x(3, g)
-        make_k3(0)
-        make_k3(1)
+            for i in range(2):
+                project_k_half(i, 2, g)
+        for h in range(2):
+            copy_p(2, h)
+        make_k3(2, 1)
+        quant_k(0, 2)
+        for h in range(2):
+            make_k2(2, h)
+        round_k2(2, 2)
+        make_k3(3, 1)
+        for g in range(2):
+            project_k_half(0, 3, g)
+        for h in range(2):
+            copy_p(3, h)
+        round_k2(4, 2)
+        for h in range(2):
+            project_bank(1, 3, h)
+        make_k2(3, 0)
+        quant_k(2, 2)
+        make_k2(3, 1)
 
-        for d in (2, 3):
-            early = 2 * (d - 2)
-            round_k2(early)
-            if d == 2:
-                for g in range(2):
-                    project_k_half(0, d, g)
-            for h in range(2):
-                if d == 3:
-                    project_bank(0, d, h)
-                copy_p(d, h)
-            round_k2(early + 1)
-            for h in range(2):
-                project_bank(1, d, h)
-                make_k2(d, h)
-            for c in (early, early + 1):
-                quant_k(c)
-            if d == 2:
-                make_k3(2)
-                make_k3(3)
-
+        make_k3(4, 2)
         for c in range(0, 4, 2):
             for s in range(2):
-                round_k2(c + 4 + s)
-                make_k3(c + 4 + s)
+                respond_linear(c + s, 0, O)
             for s in range(2):
-                quant_k(c + 4 + s)
-                respond(c + s, 0, O)
+                respond_cubic(c + s, 0, O)
                 copy_y(c + s, 0, O)
                 store_y(c + s, 1, 0, O)
+            if c == 0:
+                round_k2(6, 2)
+        make_k3(6, 1)
+        quant_k(4, 2)
+        make_k3(7, 1)
+        quant_k(6, 1)
+        quant_k(7, 1)
 
+        round_y(0, 0, 256)
+        round_y(0, 256, 256)
         for c in range(4, TILES):
             respond_linear(c, 0, 256)
         for c in range(4, TILES):
@@ -390,12 +406,10 @@ def tile_factoredcubicvolterraequalizer_x2_kernel(
             copy_y(c, 0, 256)
             if c % 2:
                 store_y(c - 1, 2, 0, 256)
-        for m0 in (0, 256):
-            round_y(0, m0, 256)
-        for m0 in (0, 256):
-            quant_y(0, m0, 256)
-        store_codes(0, 0, O)
+        quant_y(0, 0, 256)
+        quant_y(0, 256, 256)
         round_y(1, 0, 256)
+        store_codes(0, 0, O)
         quant_y(1, 0, 256)
         for c in range(4, TILES - 1):
             respond(c, 256, 256)

@@ -40,7 +40,7 @@ def tile_factoredcubicvolterraequalizer_x2_kernel(
         x_first = kept("x_first", [P, 2, 512], BF16, 2)
         x_pair = kept("x_pair", [P, 2 * N], BF16, 2)
         x_last = kept("x_last", [P, N], BF16, 2)
-        x_sorted = kept("x_sorted", [P, 512], F32, TILES // 2)
+        x_sorted = kept("x_sorted", [P, 512], F32, TILES - 2)
         xb = [kept("xb%d_" % d, [P, 2 * P, 4], BF16, 2) for d in range(PAIRS)]
         x_cod = [kept("x_cod%d_" % d, [P, 256], I32, 2) for d in range(PAIRS)]
         x_pl = [kept("x_pl%d_" % d, [P, 256], U8, 2) for d in range(PAIRS)]
@@ -120,7 +120,7 @@ def tile_factoredcubicvolterraequalizer_x2_kernel(
 
         def sort_words(c, copy=nc.vector.tensor_copy):
             copy(
-                out=x_sorted[c - 4][:].rearrange("p (g u k e) -> p g k u e", g=2, u=2, e=2),
+                out=x_sorted[c - 2][:].rearrange("p (g u k e) -> p g k u e", g=2, u=2, e=2),
                 in_=x_words(c).rearrange("p (g k e u) -> p g k u e", g=2, u=2, e=2),
             )
 
@@ -130,10 +130,8 @@ def tile_factoredcubicvolterraequalizer_x2_kernel(
             for u in range(2):
                 if d == 0:
                     in_ = x_first[g][:, half, :].bitcast(F32)[:, u::2]
-                elif d == 1:
-                    in_ = x_words(2 * d + half)[:, 256 * g + u : 256 * (g + 1) : 2]
                 else:
-                    in_ = x_sorted[2 * d + half - 4][:, (2 * g + u) * P : (2 * g + u + 1) * P]
+                    in_ = x_sorted[2 * d + half - 2][:, (2 * g + u) * P : (2 * g + u + 1) * P]
                 col = (2 * half + u) * P
                 nc.tensor.transpose(xt[d, g][:, col : col + P], in_, ident[:])
 
@@ -141,6 +139,13 @@ def tile_factoredcubicvolterraequalizer_x2_kernel(
             for half in range(2):
                 transpose_x(d, g, half)
             copy_x(d, g)
+
+        def turn_pair(d):
+            for half in range(2):
+                for g in range(2):
+                    transpose_x(d, g, half)
+            for g in range(2):
+                copy_x(d, g)
 
         def copy_x(d, g):
             nc.scalar.copy(
@@ -311,10 +316,10 @@ def tile_factoredcubicvolterraequalizer_x2_kernel(
         warm_up(2)
         for g in range(2):
             turn_x(0, g)
-        warm_up(1)
-        for g in range(2):
-            turn_x(1, g)
-        warm_up(1)
+        warm_up(2)
+        sort_words(2)
+        sort_words(3)
+        turn_pair(1)
         deal_scales(0)
         quant_x(0, 0)
         for g in range(2):
@@ -345,11 +350,7 @@ def tile_factoredcubicvolterraequalizer_x2_kernel(
         make_k2(1, 0)
         for g in range(2):
             turn_x(2, g)
-        for half in range(2):
-            for g in range(2):
-                transpose_x(3, g, half)
-        for g in range(2):
-            copy_x(3, g)
+        turn_pair(3)
         project_bank(1, 1, 1)
         quant_x(2, 0)
         make_k3(0, 1)

@@ -15,6 +15,7 @@ FLOPS = 2 * T * (N * R * 2 + N * O + R * O * 2)
 P = 128
 TILES = 8
 PAIRS = 4
+BANKS = 8
 
 
 def tile_factoredcubicvolterraequalizer_x2_kernel(
@@ -24,7 +25,7 @@ def tile_factoredcubicvolterraequalizer_x2_kernel(
     nc = tc.nc
     with ExitStack() as ctx:
         keep = ctx.enter_context(tc.tile_pool(name="keep", bufs=1))
-        psum = ctx.enter_context(tc.psum_pool(name="psum", bufs=8))
+        psum = ctx.enter_context(tc.psum_pool(name="psum", bufs=BANKS))
         ctx.enter_context(tc.manual_schedule())
 
         def kept(name, shape, dtype, count):
@@ -35,12 +36,14 @@ def tile_factoredcubicvolterraequalizer_x2_kernel(
         w_pl = kept("w_pl", [P, R], U8, 2)
         w_raw = [kept("w_raw%d_" % i, [P, R], I32, 2) for i in range(2)]
         w_cod = [[kept("w_cod%d_%d_" % (i, g), [P, 2 * P], I32, 2) for g in range(2)] for i in range(2)]
-        h_pl = keep.tile([P, O], U8, align_bytes=64)
-        h_cod = keep.tile([P, 4, O], I32, align_bytes=64)
+        h_pl = keep.tile([P, 2 * O], U8, align_bytes=64)
+        h1_cod = keep.tile([P, 2, O], I32, align_bytes=64)
+        h23_cod = kept("h23_cod", [P, O], I32, 2)
         x_first = kept("x_first", [P, 2, 512], BF16, 2)
-        x_pair = kept("x_pair", [P, 2 * N], BF16, 2)
+        x_pair = kept("x_pair", [P, 2 * N], BF16, 3)
         x_last = kept("x_last", [P, N], BF16, 2)
-        x_sorted = kept("x_sorted", [P, 512], F32, TILES - 2)
+        x_sorted = kept("x_sorted", [P, 512], F32, TILES - 4)
+        x_sorted_pair = kept("x_sorted_pair", [P, 512], F32, 2)
         xb = [kept("xb%d_" % d, [P, 2 * P, 4], BF16, 2) for d in range(PAIRS)]
         x_cod = [kept("x_cod%d_" % d, [P, 256], I32, 2) for d in range(PAIRS)]
         x_pl = [kept("x_pl%d_" % d, [P, 256], U8, 2) for d in range(PAIRS)]
@@ -61,51 +64,23 @@ def tile_factoredcubicvolterraequalizer_x2_kernel(
         x_v = [x[512 * g : 512 * g + 512, :].rearrange("(p t) k -> p t k", t=4) for g in range(2)]
         o_v = [out_0[512 * g : 512 * g + 512, :].rearrange("(p t) m -> p t m", t=4) for g in range(2)]
 
-        nc.vector.memset(zero[:].bitcast(I32), 0)
-        nc.vector.memset(warm_cod[:, 32:], 0)
-        nc.vector.memset(warm_pl[:].bitcast(I32), 0)
-        nc.vector.quantize_mx(out=warm_cod[:, 0:32].bitcast(FP8X4), scales=warm_pl[:, 0:32], in_=zero[:])
-        for plane in (w_pl_raw[0], w_pl_raw[1], h_pl):
-            nc.vector.memset(plane[:].bitcast(I32), 0)
-        make_identity(nc, ident[:])
-
-        def load_words(tile_ap, words):
-            nc.sync.dma_start(out=tile_ap, in_=words.rearrange("g p n t -> p g (n t)").bitcast(I32))
+        def as_words(words):
+            return words.rearrange("p n t -> p (n t)").bitcast(I32)
 
         def load_scales(plane, row, scales):
             passes = scales.shape[0]
             for q in range(4):
-                r0 = 32 * q + row
                 nc.sync.dma_start(
-                    out=plane[r0 : r0 + 4 * passes, :].bitcast(I32),
+                    out=plane[32 * q + row : 32 * q + row + 4 * passes, :].bitcast(I32),
                     in_=scales[:, 4 * q : 4 * q + 4, :].bitcast(I32),
                 )
 
         def load_pair(d):
             t0 = 2 * (d % 2)
-            nc.sync.dma_start(out=x_pair[d - 1][:], in_=x_v[d // 2][:, t0 : t0 + 2, :].rearrange("p t k -> p (t k)"))
+            nc.sync.dma_start(out=x_pair[d][:], in_=x_v[d // 2][:, t0 : t0 + 2, :].rearrange("p t k -> p (t k)"))
 
         def load_weight(i, words, g):
-            nc.sync.dma_start(out=w_raw[i][g][:], in_=words[g].rearrange("p n t -> p (n t)").bitcast(I32))
-
-        for g in range(2):
-            nc.sync.dma_start(out=x_first[g][:], in_=x_v[0][:, 0:2, 512 * g : 512 * (g + 1)])
-        load_pair(1)
-        load_scales(w_pl_raw[0], 0, a_scales)
-        for g in range(2):
-            load_weight(0, a_words, g)
-        load_weight(1, b_words, 0)
-        load_scales(w_pl_raw[1], 0, b_scales)
-        load_weight(1, b_words, 1)
-        load_pair(2)
-        for half in range(2):
-            nc.sync.dma_start(out=x_last[half][:], in_=x_v[1][:, 2 + half, :])
-        load_words(h_cod[:, 0:2, :], h1_words)
-        load_words(h_cod[:, 2:3, :], h2_words)
-        load_words(h_cod[:, 3:4, :], h3_words)
-        load_scales(h_pl, 0, h1_scales)
-        load_scales(h_pl, 8, h2_scales)
-        load_scales(h_pl, 12, h3_scales)
+            nc.sync.dma_start(out=w_raw[i][g][:], in_=as_words(words[g]))
 
         def bank(name):
             return psum.tile([P, 512], F32, tag="bank", name=name)
@@ -116,12 +91,18 @@ def tile_factoredcubicvolterraequalizer_x2_kernel(
             d, half = divmod(c, 2)
             if d == PAIRS - 1:
                 return x_last[half][:].bitcast(F32)
-            return x_pair[d - 1][:].bitcast(F32)[:, 512 * half : 512 * (half + 1)]
+            return x_pair[d][:].bitcast(F32)[:, 512 * half : 512 * (half + 1)]
 
         def sort_words(c, copy=nc.vector.tensor_copy):
             copy(
-                out=x_sorted[c - 2][:].rearrange("p (g u k e) -> p g k u e", g=2, u=2, e=2),
+                out=x_sorted[c - 4][:].rearrange("p (g u k e) -> p g k u e", g=2, u=2, e=2),
                 in_=x_words(c).rearrange("p (g k e u) -> p g k u e", g=2, u=2, e=2),
+            )
+
+        def sort_half(d, g):
+            nc.vector.tensor_copy(
+                out=x_sorted_pair[g][:].rearrange("p (s u k e) -> p s k u e", s=2, u=2, e=2),
+                in_=x_pair[d][:].bitcast(F32).rearrange("p (s g k e u) -> p s g k u e", s=2, g=2, u=2, e=2)[:, :, g, :, :, :],
             )
 
         def transpose_x(d, g, half):
@@ -130,8 +111,10 @@ def tile_factoredcubicvolterraequalizer_x2_kernel(
             for u in range(2):
                 if d == 0:
                     in_ = x_first[g][:, half, :].bitcast(F32)[:, u::2]
+                elif d == 1:
+                    in_ = x_sorted_pair[g][:, (2 * half + u) * P : (2 * half + u + 1) * P]
                 else:
-                    in_ = x_sorted[2 * d + half - 2][:, (2 * g + u) * P : (2 * g + u + 1) * P]
+                    in_ = x_sorted[2 * d + half - 4][:, (2 * g + u) * P : (2 * g + u + 1) * P]
                 col = (2 * half + u) * P
                 nc.tensor.transpose(xt[d, g][:, col : col + P], in_, ident[:])
 
@@ -177,7 +160,7 @@ def tile_factoredcubicvolterraequalizer_x2_kernel(
             nc.tensor.matmul_mx(
                 out=pq_bank[i, d, h][:, j * 256 : (j + 1) * 256],
                 lhsT=w_cod[i][g][h][:, j * P : (j + 1) * P].bitcast(FP8X4),
-                lhsT_scale=w_pl[i][4 * g : P, t * P : (t + 1) * P],
+                lhsT_scale=w_pl[i][4 + 4 * g : P, t * P : (t + 1) * P],
                 rhs=x_cod[d][g][:].bitcast(FP8X4),
                 rhs_scale=x_pl[d][g][:],
                 start=start,
@@ -233,17 +216,21 @@ def tile_factoredcubicvolterraequalizer_x2_kernel(
 
         def respond_passes(c, m0, width, passes):
             d, half = divmod(c, 2)
+            cols = slice(m0, m0 + width)
             stationary = [
                 (x_cod[d][g][:, half * P : (half + 1) * P], x_pl[d][g][:, half * P : (half + 1) * P]) for g in range(2)
             ] + [(k_cod[d][:, half, i * P : (i + 1) * P], k_pl[d][:, half, i * P : (i + 1) * P]) for i in range(2)]
+            moving = [(h1_cod[:, g, cols], h_pl[4 + 4 * g : P, cols]) for g in range(2)] + [
+                (h23_cod[0][:, cols], h_pl[12:P, cols]),
+                (h23_cod[1][:, cols], h_pl[4:P, O + m0 : O + m0 + width]),
+            ]
             for i in passes:
-                cod, pl = stationary[i]
                 nc.tensor.matmul_mx(
                     out=y_bank[c, m0][:, :width],
-                    lhsT=cod.bitcast(FP8X4),
-                    lhsT_scale=pl,
-                    rhs=h_cod[:, i, m0 : m0 + width].bitcast(FP8X4),
-                    rhs_scale=h_pl[4 * i : P, m0 : m0 + width],
+                    lhsT=stationary[i][0].bitcast(FP8X4),
+                    lhsT_scale=stationary[i][1],
+                    rhs=moving[i][0].bitcast(FP8X4),
+                    rhs_scale=moving[i][1],
                     start=(i == 0),
                     stop=(i == 3),
                 )
@@ -313,21 +300,49 @@ def tile_factoredcubicvolterraequalizer_x2_kernel(
                     stop=True,
                 )
 
+        nc.vector.memset(zero[:].bitcast(I32), 0)
+        nc.vector.memset(warm_cod[:, 32:], 0)
+        nc.vector.memset(warm_pl[:].bitcast(I32), 0)
+        nc.vector.quantize_mx(out=warm_cod[:, 0:32].bitcast(FP8X4), scales=warm_pl[:, 0:32], in_=zero[:])
+        for plane in w_pl_raw + [h_pl]:
+            nc.vector.memset(plane[:].bitcast(I32), 0)
+        make_identity(nc, ident[:])
+
+        for g in range(2):
+            nc.sync.dma_start(out=x_first[g][:], in_=x_v[0][:, 0:2, 512 * g : 512 * (g + 1)])
+        load_pair(1)
+        load_scales(w_pl_raw[0][:], 4, a_scales)
+        for g in range(2):
+            load_weight(0, a_words, g)
+        load_weight(1, b_words, 0)
+        load_scales(w_pl_raw[1][:], 4, b_scales)
+        load_weight(1, b_words, 1)
+        load_pair(2)
+        for half in range(2):
+            nc.sync.dma_start(out=x_last[half][:], in_=x_v[1][:, 2 + half, :])
+        nc.sync.dma_start(out=h1_cod[:], in_=h1_words.rearrange("g p n t -> p g (n t)").bitcast(I32))
+        nc.sync.dma_start(out=h23_cod[0][:], in_=as_words(h2_words[0]))
+        nc.sync.dma_start(out=h23_cod[1][:], in_=as_words(h3_words[0]))
+        load_scales(h_pl[:, 0:O], 4, h1_scales)
+        load_scales(h_pl[:, 0:O], 12, h2_scales)
+        load_scales(h_pl[:, O : 2 * O], 4, h3_scales)
+
+        warm_up(3)
+        turn_x(0, 0)
+        turn_x(0, 1)
         warm_up(2)
         for g in range(2):
-            turn_x(0, g)
-        warm_up(2)
-        sort_words(2)
-        sort_words(3)
-        turn_pair(1)
+            sort_half(1, g)
+            turn_x(1, g)
         deal_scales(0)
         quant_x(0, 0)
-        for g in range(2):
-            for h in range(2):
-                deal_words(0, g, h)
-            if g == 0:
-                quant_x(0, 1)
-            project_k_half(0, 0, g)
+        for h in range(2):
+            deal_words(0, 0, h)
+        project_k_half(0, 0, 0)
+        quant_x(0, 1)
+        for h in range(2):
+            deal_words(0, 1, h)
+        project_k_half(0, 0, 1)
         for g in range(2):
             copy_p(0, g)
             quant_x(1, g)
@@ -335,12 +350,12 @@ def tile_factoredcubicvolterraequalizer_x2_kernel(
         for h in range(2):
             deal_words(1, 0, h)
         deal_scales(1)
+        project_k_half(1, 0, 0)
         for h in range(2):
             deal_words(1, 1, h)
             copy_p(1, h)
-            project_bank(1, 0, h)
+        project_k_half(1, 0, 1)
         project_bank(1, 1, 0)
-
         sort_words(4)
         sort_words(5, nc.scalar.copy)
         sort_words(6, nc.scalar.copy)

@@ -36,7 +36,7 @@ def tile_factoredcubicvolterraequalizer_x2_kernel(
         w_pl = kept("w_pl", [P, R], U8, 2)
         w_raw = [kept("w_raw%d_" % i, [P, R], I32, 2) for i in range(2)]
         w_cod = [[kept("w_cod%d_%d_" % (i, g), [P, 2 * P], I32, 2) for g in range(2)] for i in range(2)]
-        h_pl = keep.tile([P, 2 * O], U8, align_bytes=64)
+        h_pl = keep.tile([P, O], U8, align_bytes=64)
         h1_cod = keep.tile([P, 2, O], I32, align_bytes=64)
         h23_cod = kept("h23_cod", [P, O], I32, 2)
         x_first = kept("x_first", [P, 2, 512], BF16, 2)
@@ -160,7 +160,7 @@ def tile_factoredcubicvolterraequalizer_x2_kernel(
             nc.tensor.matmul_mx(
                 out=pq_bank[i, d, h][:, j * 256 : (j + 1) * 256],
                 lhsT=w_cod[i][g][h][:, j * P : (j + 1) * P].bitcast(FP8X4),
-                lhsT_scale=w_pl[i][4 + 4 * g : P, t * P : (t + 1) * P],
+                lhsT_scale=w_pl[i][4 * g : P, t * P : (t + 1) * P],
                 rhs=x_cod[d][g][:].bitcast(FP8X4),
                 rhs_scale=x_pl[d][g][:],
                 start=start,
@@ -220,9 +220,8 @@ def tile_factoredcubicvolterraequalizer_x2_kernel(
             stationary = [
                 (x_cod[d][g][:, half * P : (half + 1) * P], x_pl[d][g][:, half * P : (half + 1) * P]) for g in range(2)
             ] + [(k_cod[d][:, half, i * P : (i + 1) * P], k_pl[d][:, half, i * P : (i + 1) * P]) for i in range(2)]
-            moving = [(h1_cod[:, g, cols], h_pl[4 + 4 * g : P, cols]) for g in range(2)] + [
-                (h23_cod[0][:, cols], h_pl[12:P, cols]),
-                (h23_cod[1][:, cols], h_pl[4:P, O + m0 : O + m0 + width]),
+            moving = [(h1_cod[:, g, cols], h_pl[4 * g : P, cols]) for g in range(2)] + [
+                (h23_cod[i][:, cols], h_pl[8 + 4 * i : P, cols]) for i in range(2)
             ]
             for i in passes:
                 nc.tensor.matmul_mx(
@@ -311,11 +310,11 @@ def tile_factoredcubicvolterraequalizer_x2_kernel(
         for g in range(2):
             nc.sync.dma_start(out=x_first[g][:], in_=x_v[0][:, 0:2, 512 * g : 512 * (g + 1)])
         load_pair(1)
-        load_scales(w_pl_raw[0][:], 4, a_scales)
+        load_scales(w_pl_raw[0][:], 0, a_scales)
         for g in range(2):
             load_weight(0, a_words, g)
         load_weight(1, b_words, 0)
-        load_scales(w_pl_raw[1][:], 4, b_scales)
+        load_scales(w_pl_raw[1][:], 0, b_scales)
         load_weight(1, b_words, 1)
         load_pair(2)
         for half in range(2):
@@ -323,9 +322,9 @@ def tile_factoredcubicvolterraequalizer_x2_kernel(
         nc.sync.dma_start(out=h1_cod[:], in_=h1_words.rearrange("g p n t -> p g (n t)").bitcast(I32))
         nc.sync.dma_start(out=h23_cod[0][:], in_=as_words(h2_words[0]))
         nc.sync.dma_start(out=h23_cod[1][:], in_=as_words(h3_words[0]))
-        load_scales(h_pl[:, 0:O], 4, h1_scales)
-        load_scales(h_pl[:, 0:O], 12, h2_scales)
-        load_scales(h_pl[:, O : 2 * O], 4, h3_scales)
+        load_scales(h_pl[:], 0, h1_scales)
+        load_scales(h_pl[:], 8, h2_scales)
+        load_scales(h_pl[:], 12, h3_scales)
 
         warm_up(3)
         turn_x(0, 0)

@@ -16,6 +16,8 @@ P = 128
 TILES = 8
 PAIRS = 4
 BANKS = 8
+HALF = O // 2
+ZERO_WORDS = 32
 
 
 def tile_factoredcubicvolterraequalizer_x2_kernel(
@@ -40,9 +42,9 @@ def tile_factoredcubicvolterraequalizer_x2_kernel(
         h1_cod = keep.tile([P, 2, O], I32, align_bytes=64)
         h23_cod = kept("h23_cod", [P, O], I32, 2)
         x_first = kept("x_first", [P, 2, 512], BF16, 2)
-        x_pair = kept("x_pair", [P, 2 * N], BF16, 3)
+        x_pair = dict(zip((1, 2), kept("x_pair", [P, 2 * N], BF16, 2)))
         x_last = kept("x_last", [P, N], BF16, 2)
-        x_sorted = kept("x_sorted", [P, 512], F32, TILES - 4)
+        x_sorted = kept("x_sorted", [P, 512], F32, TILES // 2)
         x_sorted_pair = kept("x_sorted_pair", [P, 512], F32, 2)
         xb = [kept("xb%d_" % d, [P, 2 * P, 4], BF16, 2) for d in range(PAIRS)]
         x_cod = [kept("x_cod%d_" % d, [P, 256], I32, 2) for d in range(PAIRS)]
@@ -53,26 +55,26 @@ def tile_factoredcubicvolterraequalizer_x2_kernel(
         k_cod = kept("k_cod", [P, 2, 256], I32, PAIRS)
         k_pl = kept("k_pl", [P, 2, 256], U8, PAIRS)
         y_first = keep.tile([P, 4, O], F32, align_bytes=64)
-        y_second = kept("y_second", [P, 4, 256], F32, 2)
+        y_second = kept("y_second", [P, 4, HALF], F32, 2)
         yb = kept("yb", [P, 4 * O], BF16, 2)
         y_cod = kept("y_cod", [P, O], I32, 2)
         y_pl = keep.tile([P, O], U8, align_bytes=64)
-        zero = keep.tile([P, P], BF16, align_bytes=64)
+        zero = keep.tile([P, 4 * ZERO_WORDS], BF16, align_bytes=64)
         warm_cod = keep.tile([P, 512], I32, align_bytes=64)
         warm_pl = keep.tile([P, 512], U8, align_bytes=64)
 
-        x_v = [x[512 * g : 512 * g + 512, :].rearrange("(p t) k -> p t k", t=4) for g in range(2)]
-        o_v = [out_0[512 * g : 512 * g + 512, :].rearrange("(p t) m -> p t m", t=4) for g in range(2)]
+        x_v = [x[512 * G : 512 * G + 512, :].rearrange("(p t) k -> p t k", t=4) for G in range(2)]
+        o_v = [out_0[512 * G : 512 * G + 512, :].rearrange("(p t) m -> p t m", t=4) for G in range(2)]
 
         def as_words(words):
             return words.rearrange("p n t -> p (n t)").bitcast(I32)
 
         def load_scales(plane, row, scales):
             passes = scales.shape[0]
-            for q in range(4):
+            for quad in range(4):
                 nc.sync.dma_start(
-                    out=plane[32 * q + row : 32 * q + row + 4 * passes, :].bitcast(I32),
-                    in_=scales[:, 4 * q : 4 * q + 4, :].bitcast(I32),
+                    out=plane[32 * quad + row : 32 * quad + row + 4 * passes, :].bitcast(I32),
+                    in_=scales[:, 4 * quad : 4 * quad + 4, :].bitcast(I32),
                 )
 
         def load_pair(d):
@@ -95,14 +97,15 @@ def tile_factoredcubicvolterraequalizer_x2_kernel(
 
         def sort_words(c, copy=nc.vector.tensor_copy):
             copy(
-                out=x_sorted[c - 4][:].rearrange("p (g u k e) -> p g k u e", g=2, u=2, e=2),
+                out=x_sorted[c - TILES // 2][:].rearrange("p (g u k e) -> p g k u e", g=2, u=2, e=2),
                 in_=x_words(c).rearrange("p (g k e u) -> p g k u e", g=2, u=2, e=2),
             )
 
-        def sort_half(d, g):
+        def sort_pass(g):
+            words = x_pair[1][:].bitcast(F32).rearrange("p (s g k e u) -> p s g k u e", s=2, g=2, u=2, e=2)
             nc.vector.tensor_copy(
                 out=x_sorted_pair[g][:].rearrange("p (s u k e) -> p s k u e", s=2, u=2, e=2),
-                in_=x_pair[d][:].bitcast(F32).rearrange("p (s g k e u) -> p s g k u e", s=2, g=2, u=2, e=2)[:, :, g, :, :, :],
+                in_=words[:, :, g, :, :, :],
             )
 
         def transpose_x(d, g, half):
@@ -114,7 +117,7 @@ def tile_factoredcubicvolterraequalizer_x2_kernel(
                 elif d == 1:
                     in_ = x_sorted_pair[g][:, (2 * half + u) * P : (2 * half + u + 1) * P]
                 else:
-                    in_ = x_sorted[2 * d + half - 4][:, (2 * g + u) * P : (2 * g + u + 1) * P]
+                    in_ = x_sorted[2 * d + half - TILES // 2][:, (2 * g + u) * P : (2 * g + u + 1) * P]
                 col = (2 * half + u) * P
                 nc.tensor.transpose(xt[d, g][:, col : col + P], in_, ident[:])
 
@@ -194,9 +197,9 @@ def tile_factoredcubicvolterraequalizer_x2_kernel(
             d, half = divmod(c, 2)
             return tile[d][:, :, half * P : (half + count) * P, :].rearrange("p h (s n) j -> p s n h j", s=count)
 
-        def kb_part(c, count, i):
+        def kb_part(c, count, f):
             d, half = divmod(c, 2)
-            return kb[d][:, half : half + count, i, :, :, :]
+            return kb[d][:, half : half + count, f, :, :, :]
 
         def make_k3(c, count):
             nc.vector.tensor_tensor(
@@ -211,7 +214,7 @@ def tile_factoredcubicvolterraequalizer_x2_kernel(
             nc.vector.quantize_mx(
                 out=k_cod[d][:, half : half + count, :].rearrange("p s w -> p (s w)").bitcast(FP8X4),
                 scales=k_pl[d][:, half : half + count, :].rearrange("p s w -> p (s w)"),
-                in_=kb[d][:, half : half + count, :, :, :, :].rearrange("p s i n h j -> p (s i n h j)"),
+                in_=kb[d][:, half : half + count, :, :, :, :].rearrange("p s f n h j -> p (s f n h j)"),
             )
 
         def respond_passes(c, m0, width, passes):
@@ -219,19 +222,19 @@ def tile_factoredcubicvolterraequalizer_x2_kernel(
             cols = slice(m0, m0 + width)
             stationary = [
                 (x_cod[d][g][:, half * P : (half + 1) * P], x_pl[d][g][:, half * P : (half + 1) * P]) for g in range(2)
-            ] + [(k_cod[d][:, half, i * P : (i + 1) * P], k_pl[d][:, half, i * P : (i + 1) * P]) for i in range(2)]
+            ] + [(k_cod[d][:, half, f * P : (f + 1) * P], k_pl[d][:, half, f * P : (f + 1) * P]) for f in range(2)]
             moving = [(h1_cod[:, g, cols], h_pl[4 * g : P, cols]) for g in range(2)] + [
-                (h23_cod[i][:, cols], h_pl[8 + 4 * i : P, cols]) for i in range(2)
+                (h23_cod[f][:, cols], h_pl[8 + 4 * f : P, cols]) for f in range(2)
             ]
-            for i in passes:
+            for step in passes:
                 nc.tensor.matmul_mx(
                     out=y_bank[c, m0][:, :width],
-                    lhsT=stationary[i][0].bitcast(FP8X4),
-                    lhsT_scale=stationary[i][1],
-                    rhs=moving[i][0].bitcast(FP8X4),
-                    rhs_scale=moving[i][1],
-                    start=(i == 0),
-                    stop=(i == 3),
+                    lhsT=stationary[step][0].bitcast(FP8X4),
+                    lhsT_scale=stationary[step][1],
+                    rhs=moving[step][0].bitcast(FP8X4),
+                    rhs_scale=moving[step][1],
+                    start=(step == 0),
+                    stop=(step == len(moving) - 1),
                 )
 
         def respond_linear(c, m0, width):
@@ -245,50 +248,51 @@ def tile_factoredcubicvolterraequalizer_x2_kernel(
             respond_linear(c, m0, width)
             respond_cubic(c, m0, width)
 
-        def y_sb(g, t0, t1, m0, width):
-            if g == 0:
+        def y_sb(G, t0, t1, m0, width):
+            if G == 0:
                 return y_first[:, t0:t1, m0 : m0 + width]
-            return y_second[m0 // 256][:, t0:t1, m0 % 256 : m0 % 256 + width]
+            return y_second[m0 // HALF][:, t0:t1, m0 % HALF : m0 % HALF + width]
 
         def copy_y(c, m0, width):
-            g, t = divmod(c, 4)
-            nc.scalar.copy(out=y_sb(g, t, t + 1, m0, width), in_=y_bank[c, m0][:, :width].rearrange("p (o m) -> p o m", o=1))
+            G, t = divmod(c, 4)
+            nc.scalar.copy(
+                out=y_sb(G, t, t + 1, m0, width), in_=y_bank[c, m0][:, :width].rearrange("p (o m) -> p o m", o=1)
+            )
 
         def store_y(c, count, m0, width):
-            g, t = divmod(c, 4)
-            nc.sync.dma_start(
-                out=o_v[g][:, t : t + count, m0 : m0 + width], in_=y_sb(g, t, t + count, m0, width)
+            G, t = divmod(c, 4)
+            nc.sync.dma_start(out=o_v[G][:, t : t + count, m0 : m0 + width], in_=y_sb(G, t, t + count, m0, width))
+
+        def round_y(G, m0, width):
+            nc.vector.tensor_copy(
+                out=yb[G][:, 4 * m0 : 4 * (m0 + width)].rearrange("p (m e t) -> p m t e", t=4, e=2),
+                in_=y_sb(G, 0, 4, m0, width).rearrange("p t (m e) -> p m t e", e=2),
             )
 
-        def round_y(g, m0, width, copy=nc.vector.tensor_copy):
-            copy(
-                out=yb[g][:, 4 * m0 : 4 * (m0 + width)].rearrange("p (m e t) -> p m t e", t=4, e=2),
-                in_=y_sb(g, 0, 4, m0, width).rearrange("p t (m e) -> p m t e", e=2),
-            )
-
-        def quant_y(g, m0, width):
+        def quant_y(G, m0, width):
             nc.vector.quantize_mx(
-                out=y_cod[g][:, m0 : m0 + width].bitcast(FP8X4),
-                scales=y_pl[4 * g : P, m0 : m0 + width],
-                in_=yb[g][:, 4 * m0 : 4 * (m0 + width)],
+                out=y_cod[G][:, m0 : m0 + width].bitcast(FP8X4),
+                scales=y_pl[4 * G : P, m0 : m0 + width],
+                in_=yb[G][:, 4 * m0 : 4 * (m0 + width)],
             )
 
-        def store_codes(g, m0, width):
+        def store_codes(G, m0, width):
             nc.sync.dma_start(
-                out=out_1[g].rearrange("p m t -> p (m t)")[:, 4 * m0 : 4 * (m0 + width)].bitcast(I32),
-                in_=y_cod[g][:, m0 : m0 + width],
+                out=out_1[G].rearrange("p m t -> p (m t)")[:, 4 * m0 : 4 * (m0 + width)].bitcast(I32),
+                in_=y_cod[G][:, m0 : m0 + width],
             )
 
         def store_scales():
-            for q in range(4):
-                queue = nc.sync if q % 2 else nc.scalar
+            for quad in range(4):
+                queue = nc.sync if quad % 2 else nc.scalar
                 queue.dma_start(
-                    out=out_2[:, 4 * q : 4 * q + 4, :].bitcast(I32), in_=y_pl[32 * q : 32 * q + 8, :].bitcast(I32)
+                    out=out_2[:, 4 * quad : 4 * quad + 4, :].bitcast(I32),
+                    in_=y_pl[32 * quad : 32 * quad + 8, :].bitcast(I32),
                 )
 
         def warm_up(count):
             idle_bank = bank("idle")
-            for i in range(count):
+            for _ in range(count):
                 nc.tensor.matmul_mx(
                     out=idle_bank[:],
                     lhsT=warm_cod[:, 0:P].bitcast(FP8X4),
@@ -300,9 +304,11 @@ def tile_factoredcubicvolterraequalizer_x2_kernel(
                 )
 
         nc.vector.memset(zero[:].bitcast(I32), 0)
-        nc.vector.memset(warm_cod[:, 32:], 0)
+        nc.vector.memset(warm_cod[:, ZERO_WORDS:], 0)
         nc.vector.memset(warm_pl[:].bitcast(I32), 0)
-        nc.vector.quantize_mx(out=warm_cod[:, 0:32].bitcast(FP8X4), scales=warm_pl[:, 0:32], in_=zero[:])
+        nc.vector.quantize_mx(
+            out=warm_cod[:, 0:ZERO_WORDS].bitcast(FP8X4), scales=warm_pl[:, 0:ZERO_WORDS], in_=zero[:]
+        )
         for plane in w_pl_raw + [h_pl]:
             nc.vector.memset(plane[:].bitcast(I32), 0)
         make_identity(nc, ident[:])
@@ -327,12 +333,13 @@ def tile_factoredcubicvolterraequalizer_x2_kernel(
         load_scales(h_pl[:], 12, h3_scales)
 
         warm_up(3)
-        turn_x(0, 0)
-        turn_x(0, 1)
+        for g in range(2):
+            turn_x(0, g)
         warm_up(2)
         for g in range(2):
-            sort_half(1, g)
+            sort_pass(g)
             turn_x(1, g)
+
         deal_scales(0)
         quant_x(0, 0)
         for h in range(2):
@@ -349,12 +356,12 @@ def tile_factoredcubicvolterraequalizer_x2_kernel(
         for h in range(2):
             deal_words(1, 0, h)
         deal_scales(1)
-        project_k_half(1, 0, 0)
         for h in range(2):
             deal_words(1, 1, h)
             copy_p(1, h)
-        project_k_half(1, 0, 1)
+            project_bank(1, 0, h)
         project_bank(1, 1, 0)
+
         sort_words(4)
         sort_words(5, nc.scalar.copy)
         sort_words(6, nc.scalar.copy)
@@ -366,6 +373,7 @@ def tile_factoredcubicvolterraequalizer_x2_kernel(
             turn_x(2, g)
         turn_pair(3)
         project_bank(1, 1, 1)
+
         quant_x(2, 0)
         make_k3(0, 1)
         quant_x(2, 1)
@@ -412,32 +420,34 @@ def tile_factoredcubicvolterraequalizer_x2_kernel(
         quant_k(6, 1)
         quant_k(7, 1)
 
-        round_y(0, 0, 256)
-        round_y(0, 256, 256)
+        last = TILES - 1
+        for m0 in (0, HALF):
+            round_y(0, m0, HALF)
         for c in range(4, TILES):
-            respond_linear(c, 0, 256)
+            respond_linear(c, 0, HALF)
         for c in range(4, TILES):
-            respond_cubic(c, 0, 256)
-            copy_y(c, 0, 256)
+            respond_cubic(c, 0, HALF)
+            copy_y(c, 0, HALF)
             if c % 2:
-                store_y(c - 1, 2, 0, 256)
-        quant_y(0, 0, 256)
-        quant_y(0, 256, 256)
-        round_y(1, 0, 256)
+                store_y(c - 1, 2, 0, HALF)
+        for m0 in (0, HALF):
+            quant_y(0, m0, HALF)
+        round_y(1, 0, HALF)
         store_codes(0, 0, O)
-        quant_y(1, 0, 256)
-        for c in range(4, TILES - 1):
-            respond(c, 256, 256)
-            copy_y(c, 256, 256)
-            if c == 5:
-                store_y(4, 2, 256, 256)
-        store_codes(1, 0, 256)
-        for m0 in (256, 384):
-            respond(7, m0, P)
-            copy_y(7, m0, P)
+        quant_y(1, 0, HALF)
+        for c in (4, 5):
+            respond(c, HALF, HALF)
+            copy_y(c, HALF, HALF)
+        store_y(4, 2, HALF, HALF)
+        respond(last - 1, HALF, HALF)
+        copy_y(last - 1, HALF, HALF)
+        store_codes(1, 0, HALF)
+        for m0 in (HALF, HALF + P):
+            respond(last, m0, P)
+            copy_y(last, m0, P)
             round_y(1, m0, P)
-        store_y(6, 2, 256, 256)
-        for m0 in (256, 384):
+        store_y(last - 1, 2, HALF, HALF)
+        for m0 in (HALF, HALF + P):
             quant_y(1, m0, P)
-        store_codes(1, 256, 256)
+        store_codes(1, HALF, HALF)
         store_scales()

@@ -6,6 +6,7 @@ from concourse.masks import make_identity
 F32 = mybir.dt.float32
 BF16 = mybir.dt.bfloat16
 I32 = mybir.dt.int32
+U32 = mybir.dt.uint32
 U8 = mybir.dt.uint8
 FP8X4 = mybir.dt.float8_e4m3fn_x4
 MULT = mybir.AluOpType.mult
@@ -44,8 +45,8 @@ def tile_factoredcubicvolterraequalizer_x2_kernel(
         x_first = kept("x_first", [P, 2, 512], BF16, 2)
         x_pair = dict(zip((1, 2), kept("x_pair", [P, 2 * N], BF16, 2)))
         x_last = kept("x_last", [P, N], BF16, 2)
-        x_sorted = kept("x_sorted", [P, 512], F32, TILES // 2)
-        x_sorted_pair = kept("x_sorted_pair", [P, 512], F32, 2)
+        x_sorted = kept("x_sorted", [P, 512], F32, 2)
+        x_sorted_pair = {d: kept("x_sorted_pair%d_" % d, [P, 512], F32, 2) for d in (1, 2)}
         xb = [kept("xb%d_" % d, [P, 2 * P, 4], BF16, 2) for d in range(PAIRS)]
         x_cod = [kept("x_cod%d_" % d, [P, 256], I32, 2) for d in range(PAIRS)]
         x_pl = [kept("x_pl%d_" % d, [P, 256], U8, 2) for d in range(PAIRS)]
@@ -89,22 +90,16 @@ def tile_factoredcubicvolterraequalizer_x2_kernel(
 
         xt, pq_bank, y_bank = {}, {}, {}
 
-        def x_words(c):
-            d, half = divmod(c, 2)
-            if d == PAIRS - 1:
-                return x_last[half][:].bitcast(F32)
-            return x_pair[d][:].bitcast(F32)[:, 512 * half : 512 * (half + 1)]
-
-        def sort_words(c, copy=nc.vector.tensor_copy):
-            copy(
-                out=x_sorted[c - TILES // 2][:].rearrange("p (g u k e) -> p g k u e", g=2, u=2, e=2),
-                in_=x_words(c).rearrange("p (g k e u) -> p g k u e", g=2, u=2, e=2),
+        def sort_tile(half):
+            nc.scalar.copy(
+                out=x_sorted[half][:].rearrange("p (g u k e) -> p g k u e", g=2, u=2, e=2),
+                in_=x_last[half][:].bitcast(F32).rearrange("p (g k e u) -> p g k u e", g=2, u=2, e=2),
             )
 
-        def sort_pass(g):
-            words = x_pair[1][:].bitcast(F32).rearrange("p (s g k e u) -> p s g k u e", s=2, g=2, u=2, e=2)
+        def sort_pass(d, g):
+            words = x_pair[d][:].bitcast(F32).rearrange("p (s g k e u) -> p s g k u e", s=2, g=2, u=2, e=2)
             nc.vector.tensor_copy(
-                out=x_sorted_pair[g][:].rearrange("p (s u k e) -> p s k u e", s=2, u=2, e=2),
+                out=x_sorted_pair[d][g][:].rearrange("p (s u k e) -> p s k u e", s=2, u=2, e=2),
                 in_=words[:, :, g, :, :, :],
             )
 
@@ -114,10 +109,10 @@ def tile_factoredcubicvolterraequalizer_x2_kernel(
             for u in range(2):
                 if d == 0:
                     in_ = x_first[g][:, half, :].bitcast(F32)[:, u::2]
-                elif d == 1:
-                    in_ = x_sorted_pair[g][:, (2 * half + u) * P : (2 * half + u + 1) * P]
+                elif d < PAIRS - 1:
+                    in_ = x_sorted_pair[d][g][:, (2 * half + u) * P : (2 * half + u + 1) * P]
                 else:
-                    in_ = x_sorted[2 * d + half - TILES // 2][:, (2 * g + u) * P : (2 * g + u + 1) * P]
+                    in_ = x_sorted[half][:, (2 * g + u) * P : (2 * g + u + 1) * P]
                 col = (2 * half + u) * P
                 nc.tensor.transpose(xt[d, g][:, col : col + P], in_, ident[:])
 
@@ -146,11 +141,14 @@ def tile_factoredcubicvolterraequalizer_x2_kernel(
                 in_=xb[d][g][:].rearrange("p r e -> p (r e)"),
             )
 
-        def deal_words(i, g, h):
-            nc.vector.tensor_copy(
+        def deal_words(i, g, h, copy=nc.vector.tensor_copy):
+            copy(
                 out=w_cod[i][g][h][:].rearrange("p (j m) -> p m j", j=2),
                 in_=w_raw[i][g][:].rearrange("p (m t) -> p m t", t=4)[:, :, 2 * h : 2 * h + 2],
             )
+
+        def scalar_move(out, in_):
+            nc.scalar.copy(out=out.bitcast(U32), in_=in_.bitcast(U32))
 
         def deal_scales(i):
             nc.vector.tensor_copy(
@@ -201,9 +199,12 @@ def tile_factoredcubicvolterraequalizer_x2_kernel(
             d, half = divmod(c, 2)
             return kb[d][:, half : half + count, f, :, :, :]
 
-        def make_k3(c, count):
+        def make_k3(c, count, places=slice(0, P)):
             nc.vector.tensor_tensor(
-                out=kb_part(c, count, 1), in0=tokens(k2_sb, c, count), in1=tokens(p_sb, c, count), op=MULT
+                out=kb_part(c, count, 1)[:, :, places, :, :],
+                in0=tokens(k2_sb, c, count)[:, :, places, :, :],
+                in1=tokens(p_sb, c, count)[:, :, places, :, :],
+                op=MULT,
             )
 
         def round_k2(c, count):
@@ -337,24 +338,26 @@ def tile_factoredcubicvolterraequalizer_x2_kernel(
             turn_x(0, g)
         warm_up(2)
         for g in range(2):
-            sort_pass(g)
+            sort_pass(1, g)
+        deal_words(0, 0, 0, scalar_move)
+        for g in range(2):
             turn_x(1, g)
 
         deal_scales(0)
         quant_x(0, 0)
-        for h in range(2):
-            deal_words(0, 0, h)
+        deal_words(0, 0, 1)
         project_k_half(0, 0, 0)
         quant_x(0, 1)
         for h in range(2):
             deal_words(0, 1, h)
         project_k_half(0, 0, 1)
+        deal_words(1, 0, 0, scalar_move)
+        quant_x(1, 0)
+        deal_words(1, 0, 1)
+        quant_x(1, 1)
         for g in range(2):
             copy_p(0, g)
-            quant_x(1, g)
             project_k_half(0, 1, g)
-        for h in range(2):
-            deal_words(1, 0, h)
         deal_scales(1)
         for h in range(2):
             deal_words(1, 1, h)
@@ -362,20 +365,20 @@ def tile_factoredcubicvolterraequalizer_x2_kernel(
             project_bank(1, 0, h)
         project_bank(1, 1, 0)
 
-        sort_words(4)
-        sort_words(5, nc.scalar.copy)
-        sort_words(6, nc.scalar.copy)
+        for s in range(2):
+            sort_pass(2, s)
+            sort_tile(s)
         make_k2(0, 0)
         make_k2(0, 1)
-        sort_words(7)
         make_k2(1, 0)
         for g in range(2):
             turn_x(2, g)
         turn_pair(3)
         project_bank(1, 1, 1)
 
+        make_k3(0, 1, slice(0, P // 2))
         quant_x(2, 0)
-        make_k3(0, 1)
+        make_k3(0, 1, slice(P // 2, P))
         quant_x(2, 1)
         make_k2(1, 1)
         quant_x(3, 0)

from contextlib import ExitStack

import concourse.mybir as mybir
from concourse.masks import make_identity

F32 = mybir.dt.float32
BF16 = mybir.dt.bfloat16
I32 = mybir.dt.int32
U32 = mybir.dt.uint32
U8 = mybir.dt.uint8
FP8X4 = mybir.dt.float8_e4m3fn_x4
MULT = mybir.AluOpType.mult

T, N, R, O = 1024, 1024, 512, 512
FLOPS = 2 * T * (N * R * 2 + N * O + R * O * 2)
P = 128
TILES = 8
PAIRS = 4
BANKS = 8
HALF = O // 2
ZERO_WORDS = 32


def tile_factoredcubicvolterraequalizer_x2_kernel(
    tc, x, a_words, a_scales, b_words, b_scales, h1_words, h1_scales,
    h2_words, h2_scales, h3_words, h3_scales, out_0, out_1, out_2,
):
    nc = tc.nc
    with ExitStack() as ctx:
        keep = ctx.enter_context(tc.tile_pool(name="keep", bufs=1))
        psum = ctx.enter_context(tc.psum_pool(name="psum", bufs=BANKS))
        ctx.enter_context(tc.manual_schedule())

        def kept(name, shape, dtype, count):
            return [keep.tile(shape, dtype, align_bytes=64, name="%s%d" % (name, i)) for i in range(count)]

        ident = keep.tile([P, P], F32, align_bytes=64)
        w_pl_raw = kept("w_pl_raw", [P, R], U8, 2)
        w_pl = kept("w_pl", [P, R], U8, 2)
        w_raw = [kept("w_raw%d_" % i, [P, R], I32, 2) for i in range(2)]
        w_cod = [[kept("w_cod%d_%d_" % (i, g), [P, 2 * P], I32, 2) for g in range(2)] for i in range(2)]
        h_pl = keep.tile([P, O], U8, align_bytes=64)
        h1_cod = keep.tile([P, 2, O], I32, align_bytes=64)
        h23_cod = kept("h23_cod", [P, O], I32, 2)
        x_first = kept("x_first", [P, 2, 512], BF16, 2)
        x_pair = dict(zip((1, 2), kept("x_pair", [P, 2 * N], BF16, 2)))
        x_last = kept("x_last", [P, N], BF16, 2)
        x_sorted = kept("x_sorted", [P, 512], F32, 2)
        x_sorted_pair = {d: kept("x_sorted_pair%d_" % d, [P, 512], F32, 2) for d in (1, 2)}
        xb = [kept("xb%d_" % d, [P, 2 * P, 4], BF16, 2) for d in range(PAIRS)]
        x_cod = [kept("x_cod%d_" % d, [P, 256], I32, 2) for d in range(PAIRS)]
        x_pl = [kept("x_pl%d_" % d, [P, 256], U8, 2) for d in range(PAIRS)]
        p_sb = kept("p_sb", [P, 2, 256, 2], F32, PAIRS)
        k2_sb = kept("k2_sb", [P, 2, 256, 2], F32, PAIRS)
        kb = kept("kb", [P, 2, 2, P, 2, 2], BF16, PAIRS)
        k_cod = kept("k_cod", [P, 2, 256], I32, PAIRS)
        k_pl = kept("k_pl", [P, 2, 256], U8, PAIRS)
        y_first = keep.tile([P, 4, O], F32, align_bytes=64)
        y_second = kept("y_second", [P, 4, HALF], F32, 2)
        yb = kept("yb", [P, 4 * O], BF16, 2)
        y_cod = kept("y_cod", [P, O], I32, 2)
        y_pl = keep.tile([P, O], U8, align_bytes=64)
        zero = keep.tile([P, 4 * ZERO_WORDS], BF16, align_bytes=64)
        warm_cod = keep.tile([P, 512], I32, align_bytes=64)
        warm_pl = keep.tile([P, 512], U8, align_bytes=64)

        x_v = [x[512 * G : 512 * G + 512, :].rearrange("(p t) k -> p t k", t=4) for G in range(2)]
        o_v = [out_0[512 * G : 512 * G + 512, :].rearrange("(p t) m -> p t m", t=4) for G in range(2)]

        def as_words(words):
            return words.rearrange("p n t -> p (n t)").bitcast(I32)

        def load_scales(plane, row, scales):
            passes = scales.shape[0]
            for quad in range(4):
                nc.sync.dma_start(
                    out=plane[32 * quad + row : 32 * quad + row + 4 * passes, :].bitcast(I32),
                    in_=scales[:, 4 * quad : 4 * quad + 4, :].bitcast(I32),
                )

        def load_pair(d):
            t0 = 2 * (d % 2)
            nc.sync.dma_start(out=x_pair[d][:], in_=x_v[d // 2][:, t0 : t0 + 2, :].rearrange("p t k -> p (t k)"))

        def load_weight(i, words, g):
            nc.sync.dma_start(out=w_raw[i][g][:], in_=as_words(words[g]))

        def bank(name):
            return psum.tile([P, 512], F32, tag="bank", name=name)

        xt, pq_bank, y_bank = {}, {}, {}

        def sort_tile(half):
            nc.scalar.copy(
                out=x_sorted[half][:].rearrange("p (g u k e) -> p g k u e", g=2, u=2, e=2),
                in_=x_last[half][:].bitcast(F32).rearrange("p (g k e u) -> p g k u e", g=2, u=2, e=2),
            )

        def sort_pass(d, g):
            words = x_pair[d][:].bitcast(F32).rearrange("p (s g k e u) -> p s g k u e", s=2, g=2, u=2, e=2)
            nc.vector.tensor_copy(
                out=x_sorted_pair[d][g][:].rearrange("p (s u k e) -> p s k u e", s=2, u=2, e=2),
                in_=words[:, :, g, :, :, :],
            )

        def transpose_x(d, g, half):
            if half == 0:
                xt[d, g] = bank("xt")
            for u in range(2):
                if d == 0:
                    in_ = x_first[g][:, half, :].bitcast(F32)[:, u::2]
                elif d < PAIRS - 1:
                    in_ = x_sorted_pair[d][g][:, (2 * half + u) * P : (2 * half + u + 1) * P]
                else:
                    in_ = x_sorted[half][:, (2 * g + u) * P : (2 * g + u + 1) * P]
                col = (2 * half + u) * P
                nc.tensor.transpose(xt[d, g][:, col : col + P], in_, ident[:])

        def turn_x(d, g):
            for half in range(2):
                transpose_x(d, g, half)
            copy_x(d, g)

        def turn_pair(d):
            for half in range(2):
                for g in range(2):
                    transpose_x(d, g, half)
            for g in range(2):
                copy_x(d, g)

        def copy_x(d, g):
            nc.scalar.copy(
                out=xb[d][g][:].rearrange("p r e -> p (r e)").bitcast(F32).rearrange("p (s r u) -> p s r u", s=2, u=2),
                in_=xt[d, g][:].rearrange("p (s u r) -> p s r u", s=2, u=2),
            )

        def quant_x(d, g):
            nc.vector.quantize_mx(
                out=x_cod[d][g][:].bitcast(FP8X4),
                scales=x_pl[d][g][:],
                in_=xb[d][g][:].rearrange("p r e -> p (r e)"),
            )

        def deal_words(i, g, h, copy=nc.vector.tensor_copy):
            copy(
                out=w_cod[i][g][h][:].rearrange("p (j m) -> p m j", j=2),
                in_=w_raw[i][g][:].rearrange("p (m t) -> p m t", t=4)[:, :, 2 * h : 2 * h + 2],
            )

        def scalar_move(out, in_):
            nc.scalar.copy(out=out.bitcast(U32), in_=in_.bitcast(U32))

        def deal_scales(i):
            nc.vector.tensor_copy(
                out=w_pl[i][:].rearrange("p (t m) -> p t m", t=4),
                in_=w_pl_raw[i][:].rearrange("p (m t) -> p t m", t=4),
            )

        def project_pass(i, d, t, g, start, stop):
            h, j = divmod(t, 2)
            nc.tensor.matmul_mx(
                out=pq_bank[i, d, h][:, j * 256 : (j + 1) * 256],
                lhsT=w_cod[i][g][h][:, j * P : (j + 1) * P].bitcast(FP8X4),
                lhsT_scale=w_pl[i][4 * g : P, t * P : (t + 1) * P],
                rhs=x_cod[d][g][:].bitcast(FP8X4),
                rhs_scale=x_pl[d][g][:],
                start=start,
                stop=stop,
            )

        def project_k_half(i, d, g):
            for t in range(4):
                if g == 0 and t % 2 == 0:
                    pq_bank[i, d, t // 2] = bank("pq")
                project_pass(i, d, t, g, g == 0 and t % 2 == 0, g == 1 and t % 2 == 1)

        def project_bank(i, d, h):
            pq_bank[i, d, h] = bank("pq")
            for t in (2 * h, 2 * h + 1):
                for g in range(2):
                    project_pass(i, d, t, g, g == 0, g == 1)

        def copy_p(d, h):
            nc.scalar.copy(out=p_sb[d][:, h, :, :], in_=pq_bank[0, d, h][:].rearrange("p (j n) -> p n j", j=2))

        def make_k2(d, h):
            nc.vector.tensor_tensor(
                out=k2_sb[d][:, h, :, :],
                in0=pq_bank[1, d, h][:].rearrange("p (j n) -> p n j", j=2),
                in1=p_sb[d][:, h, :, :],
                op=MULT,
            )

        def tokens(tile, c, count):
            d, half = divmod(c, 2)
            return tile[d][:, :, half * P : (half + count) * P, :].rearrange("p h (s n) j -> p s n h j", s=count)

        def kb_part(c, count, f):
            d, half = divmod(c, 2)
            return kb[d][:, half : half + count, f, :, :, :]

        def make_k3(c, count, places=slice(0, P)):
            nc.vector.tensor_tensor(
                out=kb_part(c, count, 1)[:, :, places, :, :],
                in0=tokens(k2_sb, c, count)[:, :, places, :, :],
                in1=tokens(p_sb, c, count)[:, :, places, :, :],
                op=MULT,
            )

        def round_k2(c, count):
            nc.scalar.copy(out=kb_part(c, count, 0), in_=tokens(k2_sb, c, count))

        def quant_k(c, count):
            d, half = divmod(c, 2)
            nc.vector.quantize_mx(
                out=k_cod[d][:, half : half + count, :].rearrange("p s w -> p (s w)").bitcast(FP8X4),
                scales=k_pl[d][:, half : half + count, :].rearrange("p s w -> p (s w)"),
                in_=kb[d][:, half : half + count, :, :, :, :].rearrange("p s f n h j -> p (s f n h j)"),
            )

        def respond_passes(c, m0, width, passes):
            d, half = divmod(c, 2)
            cols = slice(m0, m0 + width)
            stationary = [
                (x_cod[d][g][:, half * P : (half + 1) * P], x_pl[d][g][:, half * P : (half + 1) * P]) for g in range(2)
            ] + [(k_cod[d][:, half, f * P : (f + 1) * P], k_pl[d][:, half, f * P : (f + 1) * P]) for f in range(2)]
            moving = [(h1_cod[:, g, cols], h_pl[4 * g : P, cols]) for g in range(2)] + [
                (h23_cod[f][:, cols], h_pl[8 + 4 * f : P, cols]) for f in range(2)
            ]
            for step in passes:
                nc.tensor.matmul_mx(
                    out=y_bank[c, m0][:, :width],
                    lhsT=stationary[step][0].bitcast(FP8X4),
                    lhsT_scale=stationary[step][1],
                    rhs=moving[step][0].bitcast(FP8X4),
                    rhs_scale=moving[step][1],
                    start=(step == 0),
                    stop=(step == len(moving) - 1),
                )

        def respond_linear(c, m0, width):
            y_bank[c, m0] = bank("y")
            respond_passes(c, m0, width, (0, 1))

        def respond_cubic(c, m0, width):
            respond_passes(c, m0, width, (2, 3))

        def respond(c, m0, width):
            respond_linear(c, m0, width)
            respond_cubic(c, m0, width)

        def y_sb(G, t0, t1, m0, width):
            if G == 0:
                return y_first[:, t0:t1, m0 : m0 + width]
            return y_second[m0 // HALF][:, t0:t1, m0 % HALF : m0 % HALF + width]

        def copy_y(c, m0, width):
            G, t = divmod(c, 4)
            nc.scalar.copy(
                out=y_sb(G, t, t + 1, m0, width), in_=y_bank[c, m0][:, :width].rearrange("p (o m) -> p o m", o=1)
            )

        def store_y(c, count, m0, width):
            G, t = divmod(c, 4)
            nc.sync.dma_start(out=o_v[G][:, t : t + count, m0 : m0 + width], in_=y_sb(G, t, t + count, m0, width))

        def round_y(G, m0, width):
            nc.vector.tensor_copy(
                out=yb[G][:, 4 * m0 : 4 * (m0 + width)].rearrange("p (m e t) -> p m t e", t=4, e=2),
                in_=y_sb(G, 0, 4, m0, width).rearrange("p t (m e) -> p m t e", e=2),
            )

        def quant_y(G, m0, width):
            nc.vector.quantize_mx(
                out=y_cod[G][:, m0 : m0 + width].bitcast(FP8X4),
                scales=y_pl[4 * G : P, m0 : m0 + width],
                in_=yb[G][:, 4 * m0 : 4 * (m0 + width)],
            )

        def store_codes(G, m0, width):
            nc.sync.dma_start(
                out=out_1[G].rearrange("p m t -> p (m t)")[:, 4 * m0 : 4 * (m0 + width)].bitcast(I32),
                in_=y_cod[G][:, m0 : m0 + width],
            )

        def store_scales():
            for quad in range(4):
                queue = nc.sync if quad % 2 else nc.scalar
                queue.dma_start(
                    out=out_2[:, 4 * quad : 4 * quad + 4, :].bitcast(I32),
                    in_=y_pl[32 * quad : 32 * quad + 8, :].bitcast(I32),
                )

        def warm_up(count):
            idle_bank = bank("idle")
            for _ in range(count):
                nc.tensor.matmul_mx(
                    out=idle_bank[:],
                    lhsT=warm_cod[:, 0:P].bitcast(FP8X4),
                    lhsT_scale=warm_pl[:, 0:P],
                    rhs=warm_cod[:].bitcast(FP8X4),
                    rhs_scale=warm_pl[:],
                    start=True,
                    stop=True,
                )

        nc.vector.memset(zero[:].bitcast(I32), 0)
        nc.vector.memset(warm_cod[:, ZERO_WORDS:], 0)
        nc.vector.memset(warm_pl[:].bitcast(I32), 0)
        nc.vector.quantize_mx(
            out=warm_cod[:, 0:ZERO_WORDS].bitcast(FP8X4), scales=warm_pl[:, 0:ZERO_WORDS], in_=zero[:]
        )
        for plane in w_pl_raw + [h_pl]:
            nc.vector.memset(plane[:].bitcast(I32), 0)
        make_identity(nc, ident[:])

        for g in range(2):
            nc.sync.dma_start(out=x_first[g][:], in_=x_v[0][:, 0:2, 512 * g : 512 * (g + 1)])
        load_pair(1)
        load_scales(w_pl_raw[0][:], 0, a_scales)
        for g in range(2):
            load_weight(0, a_words, g)
        load_weight(1, b_words, 0)
        load_scales(w_pl_raw[1][:], 0, b_scales)
        load_weight(1, b_words, 1)
        load_pair(2)
        for half in range(2):
            nc.sync.dma_start(out=x_last[half][:], in_=x_v[1][:, 2 + half, :])
        nc.sync.dma_start(out=h1_cod[:], in_=h1_words.rearrange("g p n t -> p g (n t)").bitcast(I32))
        nc.sync.dma_start(out=h23_cod[0][:], in_=as_words(h2_words[0]))
        nc.sync.dma_start(out=h23_cod[1][:], in_=as_words(h3_words[0]))
        load_scales(h_pl[:], 0, h1_scales)
        load_scales(h_pl[:], 8, h2_scales)
        load_scales(h_pl[:], 12, h3_scales)

        warm_up(3)
        for g in range(2):
            turn_x(0, g)
        warm_up(2)
        for g in range(2):
            sort_pass(1, g)
        deal_words(0, 0, 0, scalar_move)
        for g in range(2):
            turn_x(1, g)

        deal_scales(0)
        quant_x(0, 0)
        deal_words(0, 0, 1)
        project_k_half(0, 0, 0)
        quant_x(0, 1)
        for h in range(2):
            deal_words(0, 1, h)
        project_k_half(0, 0, 1)
        deal_words(1, 0, 0, scalar_move)
        quant_x(1, 0)
        deal_words(1, 0, 1)
        quant_x(1, 1)
        for g in range(2):
            copy_p(0, g)
            project_k_half(0, 1, g)
        deal_scales(1)
        for h in range(2):
            deal_words(1, 1, h)
            copy_p(1, h)
            project_bank(1, 0, h)
        project_bank(1, 1, 0)

        for s in range(2):
            sort_pass(2, s)
            sort_tile(s)
        make_k2(0, 0)
        make_k2(0, 1)
        make_k2(1, 0)
        for g in range(2):
            turn_x(2, g)
        turn_pair(3)
        project_bank(1, 1, 1)

        make_k3(0, 1, slice(0, P // 2))
        quant_x(2, 0)
        make_k3(0, 1, slice(P // 2, P))
        quant_x(2, 1)
        make_k2(1, 1)
        quant_x(3, 0)
        make_k3(1, 1)
        quant_x(3, 1)
        round_k2(0, 2)
        for g in range(2):
            for i in range(2):
                project_k_half(i, 2, g)
        for h in range(2):
            copy_p(2, h)
        make_k3(2, 1)
        quant_k(0, 2)
        for h in range(2):
            make_k2(2, h)
        round_k2(2, 2)
        make_k3(3, 1)
        for g in range(2):
            project_k_half(0, 3, g)
        for h in range(2):
            copy_p(3, h)
        round_k2(4, 2)
        for h in range(2):
            project_bank(1, 3, h)
        make_k2(3, 0)
        quant_k(2, 2)
        make_k2(3, 1)

        make_k3(4, 2)
        for c in range(0, 4, 2):
            for s in range(2):
                respond_linear(c + s, 0, O)
            for s in range(2):
                respond_cubic(c + s, 0, O)
                copy_y(c + s, 0, O)
                store_y(c + s, 1, 0, O)
            if c == 0:
                round_k2(6, 2)
        make_k3(6, 1)
        quant_k(4, 2)
        make_k3(7, 1)
        quant_k(6, 1)
        quant_k(7, 1)

        last = TILES - 1
        for m0 in (0, HALF):
            round_y(0, m0, HALF)
        for c in range(4, TILES):
            respond_linear(c, 0, HALF)
        for c in range(4, TILES):
            respond_cubic(c, 0, HALF)
            copy_y(c, 0, HALF)
            if c % 2:
                store_y(c - 1, 2, 0, HALF)
        for m0 in (0, HALF):
            quant_y(0, m0, HALF)
        round_y(1, 0, HALF)
        store_codes(0, 0, O)
        quant_y(1, 0, HALF)
        for c in (4, 5):
            respond(c, HALF, HALF)
            copy_y(c, HALF, HALF)
        store_y(4, 2, HALF, HALF)
        respond(last - 1, HALF, HALF)
        copy_y(last - 1, HALF, HALF)
        store_codes(1, 0, HALF)
        for m0 in (HALF, HALF + P):
            respond(last, m0, P)
            copy_y(last, m0, P)
            round_y(1, m0, P)
        store_y(last - 1, 2, HALF, HALF)
        for m0 in (HALF, HALF + P):
            quant_y(1, m0, P)
        store_codes(1, HALF, HALF)
        store_scales()
